import numpy as np
import ml_dtypes


def mxq(x, axis, fmt="e4m3"):
    dtype, down = {"e4m3": (ml_dtypes.float8_e4m3fn, 7), "e5m2": (ml_dtypes.float8_e5m2, 14)}[fmt]
    v = np.moveaxis(np.asarray(x, np.float32).astype(ml_dtypes.bfloat16).astype(np.float64), axis, -1)
    blocks = v.reshape(v.shape[:-1] + (-1, 32))
    amax = np.abs(blocks).max(-1, keepdims=True)
    byte = np.maximum(np.where(amax > 0, np.frexp(amax)[1] - 1 + 127, 0) - down, 1)
    scale = np.exp2(byte - 127.0)
    codes = (blocks / scale).astype(np.float32).astype(dtype).astype(np.float64)
    return np.moveaxis((codes * scale).reshape(v.shape), -1, axis)


WIDE = False


def mx_kscale(k):
    if not WIDE:
        return np.ones(k)
    levels = np.array([10, -10, 5, -5, 0])
    if k % 512:
        return np.exp2(np.random.permutation(np.resize(levels, k // 32))).repeat(32)
    a = np.empty((k // 512, 16))
    for p in range(k // 512):
        a[p, :8] = np.random.permutation(np.resize(levels, 8))
        for g in range(8):
            far = levels[np.abs(levels - a[p, g]) >= 10]
            a[p, g + 8] = far[np.random.randint(len(far))]
    return np.exp2(a.ravel()).repeat(32)


def f64(x):
    return np.asarray(x).astype(np.float64)


def striped(idx):
    return np.tile(idx.reshape(-1, 16).T, (8, 1)).astype(np.uint16)


def unstriped(offs):
    return offs[:16].T.reshape(-1).astype(np.int64)


E2M1 = np.array([0.0, 0.5, 1.0, 1.5, 2.0, 3.0, 4.0, 6.0, -0.0, -0.5, -1.0, -1.5, -2.0, -3.0, -4.0, -6.0])


def pack_fp4(w):
    k, n = w.shape
    w = f64(np.asarray(w, np.float32).astype(ml_dtypes.bfloat16)).reshape(k // 32, 32, n)
    amax = np.abs(w).max(1)
    mant, ex = np.frexp(amax / 6.0)
    byte = np.clip(np.where(amax > 0, np.where(mant > 0.5, ex, ex - 1) + 127, 1), 1, 254)
    scaled = (w * np.exp2(127.0 - byte)[:, None, :]).reshape(k, n).astype(np.float32)
    c = np.ascontiguousarray(scaled.reshape(k // 512, 128, 4, n).transpose(0, 1, 3, 2)).astype(ml_dtypes.float4_e2m1fn).view(np.uint8) & 0xF
    words = (c[..., 0::2] | (c[..., 1::2] << 4)).reshape(k // 512, 128, 2 * n)
    return np.ascontiguousarray(words), np.ascontiguousarray(byte.astype(np.uint8).reshape(k // 512, 16, n))


def unpack_fp4(words, scales):
    g, _, n = scales.shape
    words = np.ascontiguousarray(words).reshape(g, 128, n, 2)
    nib = np.empty((g, 128, n, 4), np.uint8)
    nib[..., 0::2] = words & 0xF
    nib[..., 1::2] = words >> 4
    vals = E2M1[nib] * np.repeat(np.exp2(scales.astype(np.float64) - 127.0), 8, axis=1)[..., None]
    return vals.transpose(0, 1, 3, 2).reshape(g * 512, n)


K, T, S, H, N, U = 512, 2048, 512, 512, 256, 1024


def setup_inputs():
    n = np.random.standard_normal
    s = mx_kscale(K)[:, None]
    u = mx_kscale(H)
    packed_w2 = pack_fp4(n((H, N)) / np.sqrt(H) / u[:, None])
    return {
        "xT": (n((K, T)) * s).astype(np.float32),
        "w1": (n((K, H)) / np.sqrt(K) / s * u).astype(np.float32),
        "w2_words": packed_w2[0],
        "w2_scales": packed_w2[1],
        "skip": (n((H, U)) * u[:, None]).astype(np.float32),
        "offs": striped(np.random.permutation(T)[:S]),
        "cell": striped(np.random.permutation(U)[:S]),
    }


def reference(xT, w1, w2_words, w2_scales, skip, offs, cell):
    xq = mxq(f64(xT)[:, unstriped(offs)], 0, "e4m3")
    up = np.zeros((H, U))
    up[:, unstriped(cell)] = mxq(f64(w1), 0, "e4m3").T @ xq
    z = up + f64(skip)
    return unpack_fp4(w2_words, w2_scales).T @ mxq(z, 0, "e4m3")

@@ -1,0 +1,181 @@
+from contextlib import ExitStack
+
+import concourse.mybir as mybir
+
+K, T, S, H, N, U = 512, 2048, 512, 512, 256, 1024
+FLOPS = 2 * K * H * S + 2 * H * N * U
+
+F32 = mybir.dt.float32
+BF16 = mybir.dt.bfloat16
+I32 = mybir.dt.int32
+U32 = mybir.dt.uint32
+U16 = mybir.dt.uint16
+U8 = mybir.dt.uint8
+FP8X4 = mybir.dt.float8_e4m3fn_x4
+FP4X4 = mybir.dt.float4_e2m1fn_x4
+ADD = mybir.AluOpType.add
+
+P = 128
+PACK = 4
+LIST_COL = 16
+HALF = S // 2
+FIRST = 128
+CHUNK = 256
+
+
+def tile_picked_unet_none_e_kernel(tc, xT, w1, w2_words, w2_scales, skip, offs, cell, out):
+    nc = tc.nc
+    with ExitStack() as ctx:
+        keep = ctx.enter_context(tc.tile_pool(name="keep", bufs=1))
+        psum = ctx.enter_context(tc.psum_pool(name="psum", bufs=1))
+        psum_out = ctx.enter_context(tc.psum_pool(name="psum_out", bufs=2))
+
+        offs_sb = keep.tile([P, S // LIST_COL], U16, name="offs_sb")
+        cell_sb = keep.tile([P, S // LIST_COL], U16, name="cell_sb")
+        nc.sync.dma_start(offs_sb[:], offs)
+
+        x_rows = xT.rearrange("(p j) c -> p j c", j=PACK)
+        x_plane = [keep.tile([P, T], F32, name="x_plane%d" % j) for j in range(PACK)]
+        for j in range(PACK):
+            nc.sync.dma_start(out=x_plane[j][:], in_=x_rows[:, j, :])
+        w_rows = w1.rearrange("(p j) c -> p j c", j=PACK)
+        w_raw = [keep.tile([P, 2, H], F32, name="w_raw%d" % a) for a in range(2)]
+        for a in range(2):
+            nc.sync.dma_start(out=w_raw[a][:], in_=w_rows[:, 2 * a : 2 * a + 2, :])
+        nc.sync.dma_start(cell_sb[:], cell)
+        skip_rows = skip.rearrange("(p t) v -> p t v", t=PACK)
+        z_low = keep.tile([P, 2 * U], BF16, name="z_low")
+        z_high = keep.tile([P, 3 * U], BF16, name="z_high")
+        skip_plane = [
+            z_high[:, U : 3 * U].bitcast(F32) if t == 2 else keep.tile([P, U], F32, name="skip_plane%d" % t)[:]
+            for t in range(PACK)
+        ]
+        for t in range(PACK):
+            nc.sync.dma_start(out=skip_plane[t], in_=skip_rows[:, t, :])
+        w2_codes = keep.tile([P, 2 * N], U8, name="w2_codes", align_bytes=64)
+        nc.sync.dma_start(out=w2_codes[:].bitcast(I32), in_=w2_words[0].bitcast(I32))
+        w2_scale = keep.tile([P, N], U8, name="w2_scale", align_bytes=64)
+        nc.vector.memset(w2_scale[:].bitcast(I32), 0)
+        for q in range(4):
+            nc.sync.dma_start(
+                out=w2_scale[32 * q : 32 * q + 4, :].bitcast(I32),
+                in_=w2_scales[0, 4 * q : 4 * q + 4, :].bitcast(I32),
+            )
+
+        up = [keep.tile([P, U], F32, name="up%d" % t) for t in range(PACK)]
+        for t in range(PACK):
+            nc.vector.memset(up[t][:], 0.0)
+
+        x_bf = [keep.tile([P, HALF, PACK], BF16, name="x_bf%d" % a, align_bytes=64) for a in range(2)]
+        for j in range(PACK):
+            for a in range(2):
+                cols = slice(a * HALF // LIST_COL, (a + 1) * HALF // LIST_COL)
+                nc.vector.tensor_copy(x_bf[a][:, :, j], x_plane[j][:].indirect(offs_sb[:, cols]))
+        x_codes = keep.tile([P, S], U32, name="x_codes", align_bytes=64)
+        x_scale = keep.tile([P, S], U8, name="x_scale", align_bytes=64)
+        for a in range(2):
+            cols = slice(a * HALF, (a + 1) * HALF)
+            nc.vector.quantize_mx(
+                out=x_codes[:, cols].bitcast(FP8X4),
+                scales=x_scale[:, cols],
+                in_=x_bf[a][:].rearrange("p s j -> p (s j)"),
+            )
+
+        w_bf = [keep.tile([P, 2, P, PACK], BF16, name="w_bf%d" % b, align_bytes=64) for b in range(2)]
+        w_codes = keep.tile([P, H], U32, name="w_codes", align_bytes=64)
+        w_scale = keep.tile([P, H], U8, name="w_scale", align_bytes=64)
+        for b in range(2):
+            for a, copy in enumerate((nc.scalar.copy, nc.vector.tensor_copy)):
+                copy(
+                    out=w_bf[b][:, :, :, 2 * a : 2 * a + 2].rearrange("p t m j -> p m j t"),
+                    in_=w_raw[a][:].rearrange("p j (m t) -> p m j t", t=PACK)[:, :, :, 2 * b : 2 * b + 2],
+                )
+            cols = slice(2 * P * b, 2 * P * (b + 1))
+            nc.vector.quantize_mx(
+                out=w_codes[:, cols].bitcast(FP8X4),
+                scales=w_scale[:, cols],
+                in_=w_bf[b][:].rearrange("p t m j -> p (t m j)"),
+            )
+
+        pieces = [(0, 0, FIRST), (1, 0, FIRST), (0, FIRST, S), (1, FIRST, S), (2, 0, S), (3, 0, S)]
+        for t, lo, hi in pieces:
+            name = "h%d_%d" % (t, lo)
+            acc = psum.tile([P, hi - lo], F32, name=name + "_acc")
+            cuts = [lo, hi] if hi - lo in (128, 256, 512) else [lo, HALF, hi]
+            for c0, c1 in zip(cuts, cuts[1:]):
+                nc.tensor.matmul_mx(
+                    out=acc[:, c0 - lo : c1 - lo],
+                    lhsT=w_codes[:, P * t : P * (t + 1)].bitcast(FP8X4),
+                    lhsT_scale=w_scale[:, P * t : P * (t + 1)],
+                    rhs=x_codes[:, c0:c1].bitcast(FP8X4),
+                    rhs_scale=x_scale[:, c0:c1],
+                    start=True,
+                    stop=True,
+                )
+            h = keep.tile([P, hi - lo], F32, name=name)
+            nc.scalar.copy(out=h[:], in_=acc[:])
+            nc.vector.tensor_copy(up[t][:].indirect(cell_sb[:, lo // LIST_COL : hi // LIST_COL]), h[:])
+
+        z_pair = [z[:, 0 : 2 * U].rearrange("p (e v) -> p e v", e=2) for z in (z_low, z_high)]
+        for t in range(PACK - 1):
+            nc.gpsimd.tensor_tensor(out=z_pair[t // 2][:, t % 2, :], in0=up[t][:], in1=skip_plane[t], op=ADD)
+
+        chunks = U // CHUNK
+        z_bf = [keep.tile([P, CHUNK, PACK], BF16, name="z_bf%d" % c, align_bytes=64) for c in range(chunks)]
+        for c in range(chunks):
+            cells = slice(c * CHUNK, (c + 1) * CHUNK)
+            nc.scalar.copy(out=z_bf[c][:, :, 0:2], in_=z_pair[0][:, :, cells].rearrange("p e v -> p v e"))
+
+        out_rows = out.rearrange("(a p) v -> p a v", p=P)
+
+        def add_last(c):
+            cells = slice(c * CHUNK, (c + 1) * CHUNK)
+            nc.vector.tensor_tensor(out=z_pair[1][:, 1, cells], in0=up[3][:, cells], in1=skip_plane[3][:, cells], op=ADD)
+
+        def weave(c):
+            cells = slice(c * CHUNK, (c + 1) * CHUNK)
+            src = z_pair[1][:, :, cells].rearrange("p e v -> p v e")
+            if c % 2 == 0:
+                nc.scalar.copy(out=z_bf[c][:, :, 2:4], in_=src)
+            else:
+                nc.vector.tensor_copy(out=z_bf[c][:, :, 2:4], in_=src)
+
+        def finish(c):
+            cells = slice(c * CHUNK, (c + 1) * CHUNK)
+            z_codes = keep.tile([P, CHUNK], U32, name="z_codes%d" % c, align_bytes=64)
+            z_scale = keep.tile([P, CHUNK], U8, name="z_scale%d" % c, align_bytes=64)
+            nc.vector.quantize_mx(
+                out=z_codes[:].bitcast(FP8X4),
+                scales=z_scale[:],
+                in_=z_bf[c][:].rearrange("p v t -> p (v t)"),
+            )
+            acc = psum_out.tile([P, N // P, CHUNK], F32, name="out_acc")
+            for a in range(N // P):
+                nc.tensor.matmul_mx(
+                    out=acc[:, a, :],
+                    lhsT=w2_codes[:, 2 * P * a : 2 * P * (a + 1)].bitcast(FP4X4),
+                    lhsT_scale=w2_scale[:, P * a : P * (a + 1)],
+                    rhs=z_codes[:].bitcast(FP8X4),
+                    rhs_scale=z_scale[:],
+                    start=True,
+                    stop=True,
+                )
+            res = keep.tile([P, N // P, CHUNK], F32, name="res%d" % c)
+            if c == 2:
+                nc.vector.tensor_copy(out=res[:], in_=acc[:])
+            else:
+                nc.scalar.copy(out=res[:], in_=acc[:])
+            nc.sync.dma_start(out=out_rows[:, :, cells], in_=res[:])
+
+        add_last(0)
+        weave(0)
+        add_last(1)
+        weave(1)
+        add_last(2)
+        weave(2)
+        finish(1)
+        add_last(3)
+        finish(0)
+        weave(3)
+        finish(3)
+        finish(2)

@@ -20,28 +20,30 @@ PACK = 4
 LIST_COL = 16
 HALF = S // 2
 FIRST = 128
-CHUNK = 256
+CHUNKS = [128, 256, 256, 256, 128]
 
 
 def tile_picked_unet_none_e_kernel(tc, xT, w1, w2_words, w2_scales, skip, offs, cell, out):
     nc = tc.nc
     with ExitStack() as ctx:
         keep = ctx.enter_context(tc.tile_pool(name="keep", bufs=1))
-        psum = ctx.enter_context(tc.psum_pool(name="psum", bufs=1))
-        psum_out = ctx.enter_context(tc.psum_pool(name="psum_out", bufs=2))
+        psum = ctx.enter_context(tc.psum_pool(name="psum", bufs=8))
 
         offs_sb = keep.tile([P, S // LIST_COL], U16, name="offs_sb")
         cell_sb = keep.tile([P, S // LIST_COL], U16, name="cell_sb")
-        nc.sync.dma_start(offs_sb[:], offs)
 
         x_rows = xT.rearrange("(p j) c -> p j c", j=PACK)
         x_plane = [keep.tile([P, T], F32, name="x_plane%d" % j) for j in range(PACK)]
         for j in range(PACK):
             nc.sync.dma_start(out=x_plane[j][:], in_=x_rows[:, j, :])
+            if j == 0:
+                nc.sync.dma_start(offs_sb[:], offs)
         w_rows = w1.rearrange("(p j) c -> p j c", j=PACK)
         w_raw = [keep.tile([P, 2, H], F32, name="w_raw%d" % a) for a in range(2)]
-        for a in range(2):
-            nc.sync.dma_start(out=w_raw[a][:], in_=w_rows[:, 2 * a : 2 * a + 2, :])
+        nc.sync.dma_start(out=w_raw[0][:], in_=w_rows[:, 0:2, :])
+        for half in range(2):
+            cols = slice(half * H // 2, (half + 1) * H // 2)
+            nc.sync.dma_start(out=w_raw[1][:, :, cols], in_=w_rows[:, 2:4, cols])
         nc.sync.dma_start(cell_sb[:], cell)
         skip_rows = skip.rearrange("(p t) v -> p t v", t=PACK)
         z_low = keep.tile([P, 2 * U], BF16, name="z_low")
@@ -84,23 +86,34 @@ def tile_picked_unet_none_e_kernel(tc, xT, w1, w2_words, w2_scales, skip, offs, 
         w_bf = [keep.tile([P, 2, P, PACK], BF16, name="w_bf%d" % b, align_bytes=64) for b in range(2)]
         w_codes = keep.tile([P, H], U32, name="w_codes", align_bytes=64)
         w_scale = keep.tile([P, H], U8, name="w_scale", align_bytes=64)
-        for b in range(2):
-            for a, copy in enumerate((nc.scalar.copy, nc.vector.tensor_copy)):
-                copy(
-                    out=w_bf[b][:, :, :, 2 * a : 2 * a + 2].rearrange("p t m j -> p m j t"),
-                    in_=w_raw[a][:].rearrange("p j (m t) -> p m j t", t=PACK)[:, :, :, 2 * b : 2 * b + 2],
-                )
-            cols = slice(2 * P * b, 2 * P * (b + 1))
+
+        def deal(copy, a, b, m):
+            copy(
+                out=w_bf[b][:, :, m, 2 * a : 2 * a + 2].rearrange("p t m j -> p m j t"),
+                in_=w_raw[a][:].rearrange("p j (m t) -> p m j t", t=PACK)[:, m, :, 2 * b : 2 * b + 2],
+            )
+
+        def quantize_w(t0, t1):
+            cols = slice(P * t0, P * t1)
             nc.vector.quantize_mx(
                 out=w_codes[:, cols].bitcast(FP8X4),
                 scales=w_scale[:, cols],
-                in_=w_bf[b][:].rearrange("p t m j -> p (t m j)"),
+                in_=w_bf[t0 // 2][:, t0 % 2 : t0 % 2 + t1 - t0, :, :].rearrange("p t m j -> p (t m j)"),
             )
+
+        deal(nc.scalar.copy, 0, 0, slice(0, P))
+        deal(nc.scalar.copy, 1, 0, slice(0, P // 2))
+        deal(nc.scalar.copy, 0, 1, slice(0, P))
+        deal(nc.vector.tensor_copy, 1, 0, slice(P // 2, P))
+        quantize_w(0, 1)
+        deal(nc.vector.tensor_copy, 1, 1, slice(0, P))
+        quantize_w(1, 2)
+        quantize_w(2, 4)
 
         pieces = [(0, 0, FIRST), (1, 0, FIRST), (0, FIRST, S), (1, FIRST, S), (2, 0, S), (3, 0, S)]
         for t, lo, hi in pieces:
             name = "h%d_%d" % (t, lo)
-            acc = psum.tile([P, hi - lo], F32, name=name + "_acc")
+            acc = psum.tile([P, hi - lo], F32, name=name + "_acc", tag="bank")
             cuts = [lo, hi] if hi - lo in (128, 256, 512) else [lo, HALF, hi]
             for c0, c1 in zip(cuts, cuts[1:]):
                 nc.tensor.matmul_mx(
@@ -117,42 +130,48 @@ def tile_picked_unet_none_e_kernel(tc, xT, w1, w2_words, w2_scales, skip, offs, 
             nc.vector.tensor_copy(up[t][:].indirect(cell_sb[:, lo // LIST_COL : hi // LIST_COL]), h[:])
 
         z_pair = [z[:, 0 : 2 * U].rearrange("p (e v) -> p e v", e=2) for z in (z_low, z_high)]
+        starts = [sum(CHUNKS[:c]) for c in range(len(CHUNKS) + 1)]
         for t in range(PACK - 1):
-            nc.gpsimd.tensor_tensor(out=z_pair[t // 2][:, t % 2, :], in0=up[t][:], in1=skip_plane[t], op=ADD)
+            cuts = [0, starts[2], U] if t == 1 else [0, U]
+            for v0, v1 in zip(cuts, cuts[1:]):
+                nc.gpsimd.tensor_tensor(
+                    out=z_pair[t // 2][:, t % 2, v0:v1], in0=up[t][:, v0:v1], in1=skip_plane[t][:, v0:v1], op=ADD
+                )
 
-        chunks = U // CHUNK
-        z_bf = [keep.tile([P, CHUNK, PACK], BF16, name="z_bf%d" % c, align_bytes=64) for c in range(chunks)]
+        chunks = len(CHUNKS)
+        z_bf = [keep.tile([P, CHUNKS[c], PACK], BF16, name="z_bf%d" % c, align_bytes=64) for c in range(chunks)]
         for c in range(chunks):
-            cells = slice(c * CHUNK, (c + 1) * CHUNK)
+            cells = slice(starts[c], starts[c + 1])
             nc.scalar.copy(out=z_bf[c][:, :, 0:2], in_=z_pair[0][:, :, cells].rearrange("p e v -> p v e"))
 
         out_rows = out.rearrange("(a p) v -> p a v", p=P)
 
         def add_last(c):
-            cells = slice(c * CHUNK, (c + 1) * CHUNK)
+            cells = slice(starts[c], starts[c + 1])
             nc.vector.tensor_tensor(out=z_pair[1][:, 1, cells], in0=up[3][:, cells], in1=skip_plane[3][:, cells], op=ADD)
 
         def weave(c):
-            cells = slice(c * CHUNK, (c + 1) * CHUNK)
+            cells = slice(starts[c], starts[c + 1])
             src = z_pair[1][:, :, cells].rearrange("p e v -> p v e")
-            if c % 2 == 0:
+            if c % 2 == 1:
                 nc.scalar.copy(out=z_bf[c][:, :, 2:4], in_=src)
             else:
                 nc.vector.tensor_copy(out=z_bf[c][:, :, 2:4], in_=src)
 
-        def finish(c):
-            cells = slice(c * CHUNK, (c + 1) * CHUNK)
-            z_codes = keep.tile([P, CHUNK], U32, name="z_codes%d" % c, align_bytes=64)
-            z_scale = keep.tile([P, CHUNK], U8, name="z_scale%d" % c, align_bytes=64)
+        accs = {}
+
+        def multiply(c):
+            z_codes = keep.tile([P, CHUNKS[c]], U32, name="z_codes%d" % c, align_bytes=64)
+            z_scale = keep.tile([P, CHUNKS[c]], U8, name="z_scale%d" % c, align_bytes=64)
             nc.vector.quantize_mx(
                 out=z_codes[:].bitcast(FP8X4),
                 scales=z_scale[:],
                 in_=z_bf[c][:].rearrange("p v t -> p (v t)"),
             )
-            acc = psum_out.tile([P, N // P, CHUNK], F32, name="out_acc")
             for a in range(N // P):
+                accs[c, a] = psum.tile([P, CHUNKS[c]], F32, name="out_acc%d_%d" % (c, a), tag="bank")
                 nc.tensor.matmul_mx(
-                    out=acc[:, a, :],
+                    out=accs[c, a][:],
                     lhsT=w2_codes[:, 2 * P * a : 2 * P * (a + 1)].bitcast(FP4X4),
                     lhsT_scale=w2_scale[:, P * a : P * (a + 1)],
                     rhs=z_codes[:].bitcast(FP8X4),
@@ -160,22 +179,24 @@ def tile_picked_unet_none_e_kernel(tc, xT, w1, w2_words, w2_scales, skip, offs, 
                     start=True,
                     stop=True,
                 )
-            res = keep.tile([P, N // P, CHUNK], F32, name="res%d" % c)
-            if c == 2:
-                nc.vector.tensor_copy(out=res[:], in_=acc[:])
+
+        def store(c, a):
+            cells = slice(starts[c], starts[c + 1])
+            res = keep.tile([P, CHUNKS[c]], F32, name="res%d_%d" % (c, a))
+            if a == 1 and c >= 2:
+                nc.vector.tensor_copy(out=res[:], in_=accs[c, a][:])
             else:
-                nc.scalar.copy(out=res[:], in_=acc[:])
-            nc.sync.dma_start(out=out_rows[:, :, cells], in_=res[:])
+                nc.scalar.copy(out=res[:], in_=accs[c, a][:])
+            nc.sync.dma_start(out=out_rows[:, a, cells], in_=res[:])
 
         add_last(0)
-        weave(0)
-        add_last(1)
-        weave(1)
-        add_last(2)
-        weave(2)
-        finish(1)
-        add_last(3)
-        finish(0)
-        weave(3)
-        finish(3)
-        finish(2)
+        for c in range(chunks):
+            if c + 1 < chunks:
+                add_last(c + 1)
+            weave(c)
+            if c > 0:
+                multiply(c - 1)
+        multiply(chunks - 1)
+        for c in range(chunks):
+            for a in range(N // P):
+                store(c, a)

@@ -20,6 +20,7 @@ PACK = 4
 LIST_COL = 16
 HALF = S // 2
 FIRST = 128
+JOINT = 1
 CHUNKS = [128, 256, 256, 256, 128]
 
 
@@ -39,7 +40,7 @@ def tile_picked_unet_none_e_kernel(tc, xT, w1, w2_words, w2_scales, skip, offs, 
             if j == 0:
                 nc.sync.dma_start(offs_sb[:], offs)
         w_rows = w1.rearrange("(p j) c -> p j c", j=PACK)
-        w_raw = [keep.tile([P, 2, H], F32, name="w_raw%d" % a) for a in range(2)]
+        w_raw = [keep.tile([P, 2, H], F32, name="w_raw%d" % a, tag="w_raw%d" % a, align_bytes=64) for a in range(2)]
         nc.sync.dma_start(out=w_raw[0][:], in_=w_rows[:, 0:2, :])
         for half in range(2):
             cols = slice(half * H // 2, (half + 1) * H // 2)
@@ -73,15 +74,18 @@ def tile_picked_unet_none_e_kernel(tc, xT, w1, w2_words, w2_scales, skip, offs, 
             for a in range(2):
                 cols = slice(a * HALF // LIST_COL, (a + 1) * HALF // LIST_COL)
                 nc.vector.tensor_copy(x_bf[a][:, :, j], x_plane[j][:].indirect(offs_sb[:, cols]))
-        x_codes = keep.tile([P, S], U32, name="x_codes", align_bytes=64)
-        x_scale = keep.tile([P, S], U8, name="x_scale", align_bytes=64)
-        for a in range(2):
-            cols = slice(a * HALF, (a + 1) * HALF)
+        x_codes, x_scale = {}, {}
+
+        def quantize_x(a, tag):
+            x_codes[a] = keep.tile([P, HALF], U32, name="x_codes%d" % a, tag=tag, align_bytes=64)
+            x_scale[a] = keep.tile([P, HALF], U8, name="x_scale%d" % a, align_bytes=64)
             nc.vector.quantize_mx(
-                out=x_codes[:, cols].bitcast(FP8X4),
-                scales=x_scale[:, cols],
+                out=x_codes[a][:].bitcast(FP8X4),
+                scales=x_scale[a][:],
                 in_=x_bf[a][:].rearrange("p s j -> p (s j)"),
             )
+
+        quantize_x(0, "x_codes0")
 
         w_bf = [keep.tile([P, 2, P, PACK], BF16, name="w_bf%d" % b, align_bytes=64) for b in range(2)]
         w_codes = keep.tile([P, H], U32, name="w_codes", align_bytes=64)
@@ -108,20 +112,23 @@ def tile_picked_unet_none_e_kernel(tc, xT, w1, w2_words, w2_scales, skip, offs, 
         quantize_w(0, 1)
         deal(nc.vector.tensor_copy, 1, 1, slice(0, P))
         quantize_w(1, 2)
+        quantize_x(1, "w_raw1")
         quantize_w(2, 4)
 
         pieces = [(0, 0, FIRST), (1, 0, FIRST), (0, FIRST, S), (1, FIRST, S), (2, 0, S), (3, 0, S)]
         for t, lo, hi in pieces:
             name = "h%d_%d" % (t, lo)
             acc = psum.tile([P, hi - lo], F32, name=name + "_acc", tag="bank")
-            cuts = [lo, hi] if hi - lo in (128, 256, 512) else [lo, HALF, hi]
+            cuts = [lo, hi] if hi <= HALF else [lo, HALF, hi]
             for c0, c1 in zip(cuts, cuts[1:]):
+                a = c0 // HALF
+                cols = slice(c0 - a * HALF, c1 - a * HALF)
                 nc.tensor.matmul_mx(
                     out=acc[:, c0 - lo : c1 - lo],
                     lhsT=w_codes[:, P * t : P * (t + 1)].bitcast(FP8X4),
                     lhsT_scale=w_scale[:, P * t : P * (t + 1)],
-                    rhs=x_codes[:, c0:c1].bitcast(FP8X4),
-                    rhs_scale=x_scale[:, c0:c1],
+                    rhs=x_codes[a][:, cols].bitcast(FP8X4),
+                    rhs_scale=x_scale[a][:, cols],
                     start=True,
                     stop=True,
                 )
@@ -168,10 +175,19 @@ def tile_picked_unet_none_e_kernel(tc, xT, w1, w2_words, w2_scales, skip, offs, 
                 scales=z_scale[:],
                 in_=z_bf[c][:].rearrange("p v t -> p (v t)"),
             )
+            if c < JOINT:
+                both = psum.tile([P, N // P, CHUNKS[c]], F32, name="out_acc%d" % c, tag="bank")
+                accs[c] = [both[:]]
+                halves = [both[:, a, :] for a in range(N // P)]
+            else:
+                banks = [
+                    psum.tile([P, 1, CHUNKS[c]], F32, name="out_acc%d_%d" % (c, a), tag="bank") for a in range(N // P)
+                ]
+                accs[c] = [bank[:] for bank in banks]
+                halves = [bank[:, 0, :] for bank in banks]
             for a in range(N // P):
-                accs[c, a] = psum.tile([P, CHUNKS[c]], F32, name="out_acc%d_%d" % (c, a), tag="bank")
                 nc.tensor.matmul_mx(
-                    out=accs[c, a][:],
+                    out=halves[a],
                     lhsT=w2_codes[:, 2 * P * a : 2 * P * (a + 1)].bitcast(FP4X4),
                     lhsT_scale=w2_scale[:, P * a : P * (a + 1)],
                     rhs=z_codes[:].bitcast(FP8X4),
@@ -180,14 +196,17 @@ def tile_picked_unet_none_e_kernel(tc, xT, w1, w2_words, w2_scales, skip, offs, 
                     stop=True,
                 )
 
-        def store(c, a):
+        def store(c):
             cells = slice(starts[c], starts[c + 1])
-            res = keep.tile([P, CHUNKS[c]], F32, name="res%d_%d" % (c, a))
-            if a == 1 and c >= 2:
-                nc.vector.tensor_copy(out=res[:], in_=accs[c, a][:])
-            else:
-                nc.scalar.copy(out=res[:], in_=accs[c, a][:])
-            nc.sync.dma_start(out=out_rows[:, a, cells], in_=res[:])
+            res = keep.tile([P, N // P, CHUNKS[c]], F32, name="res%d" % c)
+            for a, acc in enumerate(accs[c]):
+                rows = slice(a, a + acc.shape[1])
+                copy = nc.vector.tensor_copy if a == 1 and c >= 2 else nc.scalar.copy
+                copy(out=res[:, rows, :], in_=acc)
+                if CHUNKS[c] > P:
+                    nc.sync.dma_start(out=out_rows[:, rows, cells], in_=res[:, rows, :])
+            if CHUNKS[c] == P:
+                nc.sync.dma_start(out=out_rows[:, :, cells], in_=res[:])
 
         add_last(0)
         for c in range(chunks):
@@ -198,5 +217,4 @@ def tile_picked_unet_none_e_kernel(tc, xT, w1, w2_words, w2_scales, skip, offs, 
                 multiply(c - 1)
         multiply(chunks - 1)
         for c in range(chunks):
-            for a in range(N // P):
-                store(c, a)
+            store(c)

@@ -20,8 +20,11 @@ PACK = 4
 LIST_COL = 16
 HALF = S // 2
 FIRST = 128
-JOINT = 1
-CHUNKS = [128, 256, 256, 256, 128]
+CHUNKS = [128,256,256,128,256]
+SCALAR_WEAVES = [0,2]
+VECTOR_EMPTIES = [4]
+ONE_BANK = [0,3]
+ONE_STORE = [0,3]
 
 
 def tile_picked_unet_none_e_kernel(tc, xT, w1, w2_words, w2_scales, skip, offs, cell, out):
@@ -160,7 +163,7 @@ def tile_picked_unet_none_e_kernel(tc, xT, w1, w2_words, w2_scales, skip, offs, 
         def weave(c):
             cells = slice(starts[c], starts[c + 1])
             src = z_pair[1][:, :, cells].rearrange("p e v -> p v e")
-            if c % 2 == 1:
+            if c in SCALAR_WEAVES:
                 nc.scalar.copy(out=z_bf[c][:, :, 2:4], in_=src)
             else:
                 nc.vector.tensor_copy(out=z_bf[c][:, :, 2:4], in_=src)
@@ -175,7 +178,7 @@ def tile_picked_unet_none_e_kernel(tc, xT, w1, w2_words, w2_scales, skip, offs, 
                 scales=z_scale[:],
                 in_=z_bf[c][:].rearrange("p v t -> p (v t)"),
             )
-            if c < JOINT:
+            if c in ONE_BANK:
                 both = psum.tile([P, N // P, CHUNKS[c]], F32, name="out_acc%d" % c, tag="bank")
                 accs[c] = [both[:]]
                 halves = [both[:, a, :] for a in range(N // P)]
@@ -201,20 +204,30 @@ def tile_picked_unet_none_e_kernel(tc, xT, w1, w2_words, w2_scales, skip, offs, 
             res = keep.tile([P, N // P, CHUNKS[c]], F32, name="res%d" % c)
             for a, acc in enumerate(accs[c]):
                 rows = slice(a, a + acc.shape[1])
-                copy = nc.vector.tensor_copy if a == 1 and c >= 2 else nc.scalar.copy
+                copy = nc.vector.tensor_copy if a == 1 and c in VECTOR_EMPTIES else nc.scalar.copy
                 copy(out=res[:, rows, :], in_=acc)
-                if CHUNKS[c] > P:
+                if c not in ONE_STORE:
                     nc.sync.dma_start(out=out_rows[:, rows, cells], in_=res[:, rows, :])
-            if CHUNKS[c] == P:
+            if c in ONE_STORE:
                 nc.sync.dma_start(out=out_rows[:, :, cells], in_=res[:])
 
         add_last(0)
-        for c in range(chunks):
-            if c + 1 < chunks:
-                add_last(c + 1)
-            weave(c)
-            if c > 0:
-                multiply(c - 1)
-        multiply(chunks - 1)
-        for c in range(chunks):
-            store(c)
+        add_last(1)
+        weave(0)
+        add_last(2)
+        weave(1)
+        weave(2)
+        multiply(0)
+        add_last(3)
+        multiply(1)
+        store(0)
+        add_last(4)
+        weave(3)
+        multiply(2)
+        store(1)
+        weave(4)
+        multiply(3)
+        store(2)
+        multiply(4)
+        store(3)
+        store(4)

@@ -1,6 +1,7 @@
 from contextlib import ExitStack
 
 import concourse.mybir as mybir
+from concourse.masks import make_identity
 
 K, T, S, H, N, U = 512, 2048, 512, 512, 256, 1024
 FLOPS = 2 * K * H * S + 2 * H * N * U
@@ -31,7 +32,8 @@ def tile_picked_unet_none_e_kernel(tc, xT, w1, w2_words, w2_scales, skip, offs, 
     nc = tc.nc
     with ExitStack() as ctx:
         keep = ctx.enter_context(tc.tile_pool(name="keep", bufs=1))
-        psum = ctx.enter_context(tc.psum_pool(name="psum", bufs=8))
+        psum = ctx.enter_context(tc.psum_pool(name="psum", bufs=6))
+        held = ctx.enter_context(tc.psum_pool(name="held", bufs=1))
 
         offs_sb = keep.tile([P, S // LIST_COL], U16, name="offs_sb")
         cell_sb = keep.tile([P, S // LIST_COL], U16, name="cell_sb")
@@ -56,7 +58,7 @@ def tile_picked_unet_none_e_kernel(tc, xT, w1, w2_words, w2_scales, skip, offs, 
             z_high[:, U : 3 * U].bitcast(F32) if t == 2 else keep.tile([P, U], F32, name="skip_plane%d" % t)[:]
             for t in range(PACK)
         ]
-        for t in range(PACK):
+        for t in (3, 0, 1, 2):
             nc.sync.dma_start(out=skip_plane[t], in_=skip_rows[:, t, :])
         w2_codes = keep.tile([P, 2 * N], U8, name="w2_codes", align_bytes=64)
         nc.sync.dma_start(out=w2_codes[:].bitcast(I32), in_=w2_words[0].bitcast(I32))
@@ -139,6 +141,20 @@ def tile_picked_unet_none_e_kernel(tc, xT, w1, w2_words, w2_scales, skip, offs, 
             nc.scalar.copy(out=h[:], in_=acc[:])
             nc.vector.tensor_copy(up[t][:].indirect(cell_sb[:, lo // LIST_COL : hi // LIST_COL]), h[:])
 
+        ident = keep.tile([P, P], F32, name="ident")
+        make_identity(nc, ident[:])
+        skip_bank = []
+        for b, (g0, g1) in enumerate([(0, 1), (1, 5)]):
+            turned = psum.tile([P, g1 - g0, P], F32, name="turned%d" % b, tag="bank")
+            for g in range(g0, g1):
+                nc.tensor.transpose(turned[:, g - g0, :], skip_plane[3][:, g * P : (g + 1) * P], ident[:])
+            turned_sb = keep.tile([P, g1 - g0, P], F32, name="turned_sb%d" % b)
+            nc.scalar.copy(out=turned_sb[:], in_=turned[:])
+            bank = held.tile([P, (g1 - g0) * P], F32, name="skip_bank%d" % b, tag="held%d" % b)
+            for g in range(g1 - g0):
+                nc.tensor.transpose(bank[:, g * P : (g + 1) * P], turned_sb[:, g, :], ident[:])
+            skip_bank.append(bank)
+
         z_pair = [z[:, 0 : 2 * U].rearrange("p (e v) -> p e v", e=2) for z in (z_low, z_high)]
         starts = [sum(CHUNKS[:c]) for c in range(len(CHUNKS) + 1)]
         for t in range(PACK - 1):
@@ -158,7 +174,28 @@ def tile_picked_unet_none_e_kernel(tc, xT, w1, w2_words, w2_scales, skip, offs, 
 
         def add_last(c):
             cells = slice(starts[c], starts[c + 1])
-            nc.vector.tensor_tensor(out=z_pair[1][:, 1, cells], in0=up[3][:, cells], in1=skip_plane[3][:, cells], op=ADD)
+            if c == 3:
+                cells = slice(starts[3], U)
+                nc.gpsimd.tensor_tensor(
+                    out=z_pair[1][:, 1, cells], in0=up[3][:, cells], in1=skip_plane[3][:, cells], op=ADD
+                )
+            else:
+                b, v0 = (0, 0) if c == 0 else (1, starts[c] - P)
+                nc.vector.tensor_tensor(
+                    out=z_pair[1][:, 1, cells], in0=up[3][:, cells], in1=skip_bank[b][:, v0 : v0 + CHUNKS[c]], op=ADD
+                )
+            if c == 0:
+                warm = held.tile([P, H], F32, name="warm", tag="held0")
+                for a in range(2):
+                    nc.tensor.matmul_mx(
+                        out=warm[:],
+                        lhsT=x_codes[a][:, 0:P].bitcast(FP8X4),
+                        lhsT_scale=x_scale[a][:, 0:P],
+                        rhs=w_codes[:].bitcast(FP8X4),
+                        rhs_scale=w_scale[:],
+                        start=True,
+                        stop=True,
+                    )
 
         def weave(c):
             cells = slice(starts[c], starts[c + 1])
@@ -211,6 +248,7 @@ def tile_picked_unet_none_e_kernel(tc, xT, w1, w2_words, w2_scales, skip, offs, 
             if c in ONE_STORE:
                 nc.sync.dma_start(out=out_rows[:, :, cells], in_=res[:])
 
+        add_last(3)
         add_last(0)
         add_last(1)
         weave(0)
@@ -218,10 +256,8 @@ def tile_picked_unet_none_e_kernel(tc, xT, w1, w2_words, w2_scales, skip, offs, 
         weave(1)
         weave(2)
         multiply(0)
-        add_last(3)
         multiply(1)
         store(0)
-        add_last(4)
         weave(3)
         multiply(2)
         store(1)

@@ -32,7 +32,7 @@ def tile_picked_unet_none_e_kernel(tc, xT, w1, w2_words, w2_scales, skip, offs, 
     nc = tc.nc
     with ExitStack() as ctx:
         keep = ctx.enter_context(tc.tile_pool(name="keep", bufs=1))
-        psum = ctx.enter_context(tc.psum_pool(name="psum", bufs=6))
+        psum = ctx.enter_context(tc.psum_pool(name="psum", bufs=7))
         held = ctx.enter_context(tc.psum_pool(name="held", bufs=1))
 
         offs_sb = keep.tile([P, S // LIST_COL], U16, name="offs_sb")
@@ -144,7 +144,7 @@ def tile_picked_unet_none_e_kernel(tc, xT, w1, w2_words, w2_scales, skip, offs, 
         ident = keep.tile([P, P], F32, name="ident")
         make_identity(nc, ident[:])
         skip_bank = []
-        for b, (g0, g1) in enumerate([(0, 1), (1, 5)]):
+        for b, (g0, g1) in enumerate([(0, 1)]):
             turned = psum.tile([P, g1 - g0, P], F32, name="turned%d" % b, tag="bank")
             for g in range(g0, g1):
                 nc.tensor.transpose(turned[:, g - g0, :], skip_plane[3][:, g * P : (g + 1) * P], ident[:])
@@ -174,16 +174,8 @@ def tile_picked_unet_none_e_kernel(tc, xT, w1, w2_words, w2_scales, skip, offs, 
 
         def add_last(c):
             cells = slice(starts[c], starts[c + 1])
-            if c == 3:
-                cells = slice(starts[3], U)
-                nc.gpsimd.tensor_tensor(
-                    out=z_pair[1][:, 1, cells], in0=up[3][:, cells], in1=skip_plane[3][:, cells], op=ADD
-                )
-            else:
-                b, v0 = (0, 0) if c == 0 else (1, starts[c] - P)
-                nc.vector.tensor_tensor(
-                    out=z_pair[1][:, 1, cells], in0=up[3][:, cells], in1=skip_bank[b][:, v0 : v0 + CHUNKS[c]], op=ADD
-                )
+            other = skip_bank[0][:] if c == 0 else skip_plane[3][:, cells]
+            nc.vector.tensor_tensor(out=z_pair[1][:, 1, cells], in0=up[3][:, cells], in1=other, op=ADD)
             if c == 0:
                 warm = held.tile([P, H], F32, name="warm", tag="held0")
                 for a in range(2):
@@ -248,7 +240,6 @@ def tile_picked_unet_none_e_kernel(tc, xT, w1, w2_words, w2_scales, skip, offs, 
             if c in ONE_STORE:
                 nc.sync.dma_start(out=out_rows[:, :, cells], in_=res[:])
 
-        add_last(3)
         add_last(0)
         add_last(1)
         weave(0)
@@ -256,8 +247,10 @@ def tile_picked_unet_none_e_kernel(tc, xT, w1, w2_words, w2_scales, skip, offs, 
         weave(1)
         weave(2)
         multiply(0)
+        add_last(3)
         multiply(1)
         store(0)
+        add_last(4)
         weave(3)
         multiply(2)
         store(1)

@@ -19,20 +19,22 @@ ADD = mybir.AluOpType.add
 P = 128
 PACK = 4
 LIST_COL = 16
+QUADRANT = 32
+BANKS = 8
 HALF = S // 2
 FIRST = 128
-CHUNKS = [128,256,256,128,256]
-SCALAR_WEAVES = [0,2]
-VECTOR_EMPTIES = [4]
-ONE_BANK = [0,3]
-ONE_STORE = [0,3]
+WARM_UPS = 2
+
+NARROW, WIDE = 128, 256
+CHUNKS = [NARROW, WIDE, WIDE, NARROW, WIDE]
+SCALAR_WEAVES_BELOW = 3
 
 
 def tile_picked_unet_none_e_kernel(tc, xT, w1, w2_words, w2_scales, skip, offs, cell, out):
     nc = tc.nc
     with ExitStack() as ctx:
         keep = ctx.enter_context(tc.tile_pool(name="keep", bufs=1))
-        psum = ctx.enter_context(tc.psum_pool(name="psum", bufs=7))
+        psum = ctx.enter_context(tc.psum_pool(name="psum", bufs=BANKS - 1))
         held = ctx.enter_context(tc.psum_pool(name="held", bufs=1))
 
         offs_sb = keep.tile([P, S // LIST_COL], U16, name="offs_sb")
@@ -51,6 +53,7 @@ def tile_picked_unet_none_e_kernel(tc, xT, w1, w2_words, w2_scales, skip, offs, 
             cols = slice(half * H // 2, (half + 1) * H // 2)
             nc.sync.dma_start(out=w_raw[1][:, :, cols], in_=w_rows[:, 2:4, cols])
         nc.sync.dma_start(cell_sb[:], cell)
+
         skip_rows = skip.rearrange("(p t) v -> p t v", t=PACK)
         z_low = keep.tile([P, 2 * U], BF16, name="z_low")
         z_high = keep.tile([P, 3 * U], BF16, name="z_high")
@@ -58,15 +61,15 @@ def tile_picked_unet_none_e_kernel(tc, xT, w1, w2_words, w2_scales, skip, offs, 
             z_high[:, U : 3 * U].bitcast(F32) if t == 2 else keep.tile([P, U], F32, name="skip_plane%d" % t)[:]
             for t in range(PACK)
         ]
-        for t in (3, 0, 1, 2):
+        for t in [PACK - 1] + list(range(PACK - 1)):
             nc.sync.dma_start(out=skip_plane[t], in_=skip_rows[:, t, :])
         w2_codes = keep.tile([P, 2 * N], U8, name="w2_codes", align_bytes=64)
         nc.sync.dma_start(out=w2_codes[:].bitcast(I32), in_=w2_words[0].bitcast(I32))
         w2_scale = keep.tile([P, N], U8, name="w2_scale", align_bytes=64)
         nc.vector.memset(w2_scale[:].bitcast(I32), 0)
-        for q in range(4):
+        for q in range(P // QUADRANT):
             nc.sync.dma_start(
-                out=w2_scale[32 * q : 32 * q + 4, :].bitcast(I32),
+                out=w2_scale[QUADRANT * q : QUADRANT * q + 4, :].bitcast(I32),
                 in_=w2_scales[0, 4 * q : 4 * q + 4, :].bitcast(I32),
             )
 
@@ -98,8 +101,8 @@ def tile_picked_unet_none_e_kernel(tc, xT, w1, w2_words, w2_scales, skip, offs, 
 
         def deal(copy, a, b, m):
             copy(
-                out=w_bf[b][:, :, m, 2 * a : 2 * a + 2].rearrange("p t m j -> p m j t"),
-                in_=w_raw[a][:].rearrange("p j (m t) -> p m j t", t=PACK)[:, m, :, 2 * b : 2 * b + 2],
+                out=w_bf[b][:, :, m, 2 * a : 2 * a + 2].rearrange("p t m j -> p m t j"),
+                in_=w_raw[a][:].rearrange("p j (m t) -> p m t j", t=PACK)[:, m, 2 * b : 2 * b + 2, :],
             )
 
         def quantize_w(t0, t1):
@@ -120,7 +123,7 @@ def tile_picked_unet_none_e_kernel(tc, xT, w1, w2_words, w2_scales, skip, offs, 
         quantize_x(1, "w_raw1")
         quantize_w(2, 4)
 
-        pieces = [(0, 0, FIRST), (1, 0, FIRST), (0, FIRST, S), (1, FIRST, S), (2, 0, S), (3, 0, S)]
+        pieces = [(t, 0, FIRST) for t in range(2)] + [(t, FIRST, S) for t in range(2)] + [(t, 0, S) for t in range(2, PACK)]
         for t, lo, hi in pieces:
             name = "h%d_%d" % (t, lo)
             acc = psum.tile([P, hi - lo], F32, name=name + "_acc", tag="bank")
@@ -143,20 +146,16 @@ def tile_picked_unet_none_e_kernel(tc, xT, w1, w2_words, w2_scales, skip, offs, 
 
         ident = keep.tile([P, P], F32, name="ident")
         make_identity(nc, ident[:])
-        skip_bank = []
-        for b, (g0, g1) in enumerate([(0, 1)]):
-            turned = psum.tile([P, g1 - g0, P], F32, name="turned%d" % b, tag="bank")
-            for g in range(g0, g1):
-                nc.tensor.transpose(turned[:, g - g0, :], skip_plane[3][:, g * P : (g + 1) * P], ident[:])
-            turned_sb = keep.tile([P, g1 - g0, P], F32, name="turned_sb%d" % b)
-            nc.scalar.copy(out=turned_sb[:], in_=turned[:])
-            bank = held.tile([P, (g1 - g0) * P], F32, name="skip_bank%d" % b, tag="held%d" % b)
-            for g in range(g1 - g0):
-                nc.tensor.transpose(bank[:, g * P : (g + 1) * P], turned_sb[:, g, :], ident[:])
-            skip_bank.append(bank)
+        turned = psum.tile([P, NARROW], F32, name="turned", tag="bank")
+        nc.tensor.transpose(turned[:], skip_plane[3][:, 0:NARROW], ident[:])
+        turned_sb = keep.tile([P, NARROW], F32, name="turned_sb")
+        nc.scalar.copy(out=turned_sb[:], in_=turned[:])
+        skip_first = held.tile([P, NARROW], F32, name="skip_first", tag="held")
+        nc.tensor.transpose(skip_first[:], turned_sb[:], ident[:])
 
+        chunks = len(CHUNKS)
+        starts = [sum(CHUNKS[:c]) for c in range(chunks + 1)]
         z_pair = [z[:, 0 : 2 * U].rearrange("p (e v) -> p e v", e=2) for z in (z_low, z_high)]
-        starts = [sum(CHUNKS[:c]) for c in range(len(CHUNKS) + 1)]
         for t in range(PACK - 1):
             cuts = [0, starts[2], U] if t == 1 else [0, U]
             for v0, v1 in zip(cuts, cuts[1:]):
@@ -164,7 +163,6 @@ def tile_picked_unet_none_e_kernel(tc, xT, w1, w2_words, w2_scales, skip, offs, 
                     out=z_pair[t // 2][:, t % 2, v0:v1], in0=up[t][:, v0:v1], in1=skip_plane[t][:, v0:v1], op=ADD
                 )
 
-        chunks = len(CHUNKS)
         z_bf = [keep.tile([P, CHUNKS[c], PACK], BF16, name="z_bf%d" % c, align_bytes=64) for c in range(chunks)]
         for c in range(chunks):
             cells = slice(starts[c], starts[c + 1])
@@ -172,30 +170,29 @@ def tile_picked_unet_none_e_kernel(tc, xT, w1, w2_words, w2_scales, skip, offs, 
 
         out_rows = out.rearrange("(a p) v -> p a v", p=P)
 
+        def warm_up():
+            warm = held.tile([P, H], F32, name="warm", tag="held")
+            for a in range(WARM_UPS):
+                nc.tensor.matmul_mx(
+                    out=warm[:],
+                    lhsT=x_codes[a][:, 0:P].bitcast(FP8X4),
+                    lhsT_scale=x_scale[a][:, 0:P],
+                    rhs=w_codes[:].bitcast(FP8X4),
+                    rhs_scale=w_scale[:],
+                    start=True,
+                    stop=True,
+                )
+
         def add_last(c):
             cells = slice(starts[c], starts[c + 1])
-            other = skip_bank[0][:] if c == 0 else skip_plane[3][:, cells]
+            other = skip_first[:] if c == 0 else skip_plane[3][:, cells]
             nc.vector.tensor_tensor(out=z_pair[1][:, 1, cells], in0=up[3][:, cells], in1=other, op=ADD)
-            if c == 0:
-                warm = held.tile([P, H], F32, name="warm", tag="held0")
-                for a in range(2):
-                    nc.tensor.matmul_mx(
-                        out=warm[:],
-                        lhsT=x_codes[a][:, 0:P].bitcast(FP8X4),
-                        lhsT_scale=x_scale[a][:, 0:P],
-                        rhs=w_codes[:].bitcast(FP8X4),
-                        rhs_scale=w_scale[:],
-                        start=True,
-                        stop=True,
-                    )
 
         def weave(c):
             cells = slice(starts[c], starts[c + 1])
-            src = z_pair[1][:, :, cells].rearrange("p e v -> p v e")
-            if c in SCALAR_WEAVES:
-                nc.scalar.copy(out=z_bf[c][:, :, 2:4], in_=src)
-            else:
-                nc.vector.tensor_copy(out=z_bf[c][:, :, 2:4], in_=src)
+            on_scalar = c % 2 == 0 and c < SCALAR_WEAVES_BELOW
+            copy = nc.scalar.copy if on_scalar else nc.vector.tensor_copy
+            copy(out=z_bf[c][:, :, 2:4], in_=z_pair[1][:, :, cells].rearrange("p e v -> p v e"))
 
         accs = {}
 
@@ -207,19 +204,19 @@ def tile_picked_unet_none_e_kernel(tc, xT, w1, w2_words, w2_scales, skip, offs, 
                 scales=z_scale[:],
                 in_=z_bf[c][:].rearrange("p v t -> p (v t)"),
             )
-            if c in ONE_BANK:
+            if CHUNKS[c] == NARROW:
                 both = psum.tile([P, N // P, CHUNKS[c]], F32, name="out_acc%d" % c, tag="bank")
                 accs[c] = [both[:]]
-                halves = [both[:, a, :] for a in range(N // P)]
+                blocks = [both[:, a, :] for a in range(N // P)]
             else:
                 banks = [
                     psum.tile([P, 1, CHUNKS[c]], F32, name="out_acc%d_%d" % (c, a), tag="bank") for a in range(N // P)
                 ]
                 accs[c] = [bank[:] for bank in banks]
-                halves = [bank[:, 0, :] for bank in banks]
+                blocks = [bank[:, 0, :] for bank in banks]
             for a in range(N // P):
                 nc.tensor.matmul_mx(
-                    out=halves[a],
+                    out=blocks[a],
                     lhsT=w2_codes[:, 2 * P * a : 2 * P * (a + 1)].bitcast(FP4X4),
                     lhsT_scale=w2_scale[:, P * a : P * (a + 1)],
                     rhs=z_codes[:].bitcast(FP8X4),
@@ -233,30 +230,20 @@ def tile_picked_unet_none_e_kernel(tc, xT, w1, w2_words, w2_scales, skip, offs, 
             res = keep.tile([P, N // P, CHUNKS[c]], F32, name="res%d" % c)
             for a, acc in enumerate(accs[c]):
                 rows = slice(a, a + acc.shape[1])
-                copy = nc.vector.tensor_copy if a == 1 and c in VECTOR_EMPTIES else nc.scalar.copy
+                copy = nc.vector.tensor_copy if (c, a) == (chunks - 1, N // P - 1) else nc.scalar.copy
                 copy(out=res[:, rows, :], in_=acc)
-                if c not in ONE_STORE:
-                    nc.sync.dma_start(out=out_rows[:, rows, cells], in_=res[:, rows, :])
-            if c in ONE_STORE:
-                nc.sync.dma_start(out=out_rows[:, :, cells], in_=res[:])
+                nc.sync.dma_start(out=out_rows[:, rows, cells], in_=res[:, rows, :])
 
         add_last(0)
+        warm_up()
         add_last(1)
         weave(0)
-        add_last(2)
-        weave(1)
-        weave(2)
-        multiply(0)
-        add_last(3)
-        multiply(1)
-        store(0)
-        add_last(4)
-        weave(3)
-        multiply(2)
-        store(1)
-        weave(4)
-        multiply(3)
-        store(2)
-        multiply(4)
-        store(3)
-        store(4)
+        for c in range(chunks):
+            if c + 2 < chunks:
+                add_last(c + 2)
+            if c + 1 < chunks:
+                weave(c + 1)
+            multiply(c)
+            if c > 0:
+                store(c - 1)
+        store(chunks - 1)

@@ -23,6 +23,7 @@ QUADRANT = 32
 BANKS = 8
 HALF = S // 2
 FIRST = 128
+PIECE = 256
 WARM_UPS = 2
 
 NARROW, WIDE = 128, 256
@@ -47,22 +48,22 @@ def tile_picked_unet_none_e_kernel(tc, xT, w1, w2_words, w2_scales, skip, offs, 
             if j == 0:
                 nc.sync.dma_start(offs_sb[:], offs)
         w_rows = w1.rearrange("(p j) c -> p j c", j=PACK)
-        w_raw = [keep.tile([P, 2, H], F32, name="w_raw%d" % a, tag="w_raw%d" % a, align_bytes=64) for a in range(2)]
-        nc.sync.dma_start(out=w_raw[0][:], in_=w_rows[:, 0:2, :])
-        for half in range(2):
-            cols = slice(half * H // 2, (half + 1) * H // 2)
-            nc.sync.dma_start(out=w_raw[1][:, :, cols], in_=w_rows[:, 2:4, cols])
+        w_raw = [keep.tile([P, PACK, H // 2], F32, name="w_raw%d" % a) for a in range(2)]
+        for a in range(2):
+            nc.sync.dma_start(out=w_raw[a][:], in_=w_rows[:, :, a * H // 2 : (a + 1) * H // 2])
         nc.sync.dma_start(cell_sb[:], cell)
 
         skip_rows = skip.rearrange("(p t) v -> p t v", t=PACK)
-        z_low = keep.tile([P, 2 * U], BF16, name="z_low")
-        z_high = keep.tile([P, 3 * U], BF16, name="z_high")
-        skip_plane = [
-            z_high[:, U : 3 * U].bitcast(F32) if t == 2 else keep.tile([P, U], F32, name="skip_plane%d" % t)[:]
-            for t in range(PACK)
-        ]
-        for t in [PACK - 1] + list(range(PACK - 1)):
-            nc.sync.dma_start(out=skip_plane[t], in_=skip_rows[:, t, :])
+        z_high = keep.tile([P, 2, U], BF16, name="z_high")
+        z_low = [keep.tile([P, 2, PIECE], BF16, name="z_low%d" % a)[:] for a in range(U // PIECE - 1)]
+        z_low.append(z_high[:, 1, :].rearrange("p (e v) -> p e v", e=2)[:, :, NARROW // 2 : NARROW // 2 + PIECE])
+        skip_plane = [keep.tile([P, U], F32, name="skip_plane%d" % t)[:] for t in range(PACK)]
+        low, high = slice(0, P // 2), slice(P // 2, P)
+        nc.sync.dma_start(out=skip_plane[3], in_=skip_rows[:, 3, :])
+        for a, rows in enumerate([low, high]):
+            for e, part in enumerate([low, high]):
+                nc.sync.dma_start(out=skip_plane[a][part, :], in_=skip_rows[rows, e, :])
+        nc.sync.dma_start(out=skip_plane[2], in_=skip_rows[:, 2, :])
         w2_codes = keep.tile([P, 2 * N], U8, name="w2_codes", align_bytes=64)
         nc.sync.dma_start(out=w2_codes[:].bitcast(I32), in_=w2_words[0].bitcast(I32))
         w2_scale = keep.tile([P, N], U8, name="w2_scale", align_bytes=64)
@@ -82,49 +83,48 @@ def tile_picked_unet_none_e_kernel(tc, xT, w1, w2_words, w2_scales, skip, offs, 
             for a in range(2):
                 cols = slice(a * HALF // LIST_COL, (a + 1) * HALF // LIST_COL)
                 nc.vector.tensor_copy(x_bf[a][:, :, j], x_plane[j][:].indirect(offs_sb[:, cols]))
-        x_codes, x_scale = {}, {}
-
-        def quantize_x(a, tag):
-            x_codes[a] = keep.tile([P, HALF], U32, name="x_codes%d" % a, tag=tag, align_bytes=64)
-            x_scale[a] = keep.tile([P, HALF], U8, name="x_scale%d" % a, align_bytes=64)
+        x_codes = [keep.tile([P, HALF], U32, name="x_codes%d" % a, align_bytes=64) for a in range(2)]
+        x_scale = [keep.tile([P, HALF], U8, name="x_scale%d" % a, align_bytes=64) for a in range(2)]
+        for a in range(2):
             nc.vector.quantize_mx(
                 out=x_codes[a][:].bitcast(FP8X4),
                 scales=x_scale[a][:],
                 in_=x_bf[a][:].rearrange("p s j -> p (s j)"),
             )
 
-        quantize_x(0, "x_codes0")
-
-        w_bf = [keep.tile([P, 2, P, PACK], BF16, name="w_bf%d" % b, align_bytes=64) for b in range(2)]
+        w_mixed = {}
+        w_plain = keep.tile([P, 2, P, PACK], BF16, name="w_plain", align_bytes=64)
         w_codes = keep.tile([P, H], U32, name="w_codes", align_bytes=64)
         w_scale = keep.tile([P, H], U8, name="w_scale", align_bytes=64)
 
-        def deal(copy, a, b, m):
+        def deal(copy, dst, a, b):
             copy(
-                out=w_bf[b][:, :, m, 2 * a : 2 * a + 2].rearrange("p t m j -> p m t j"),
-                in_=w_raw[a][:].rearrange("p j (m t) -> p m t j", t=PACK)[:, m, 2 * b : 2 * b + 2, :],
+                out=dst.rearrange("p t m j -> p m t j"),
+                in_=w_raw[a][:].rearrange("p j (m t) -> p m t j", t=PACK)[:, :, 2 * b : 2 * b + 2, :],
             )
 
-        def quantize_w(t0, t1):
-            cols = slice(P * t0, P * t1)
-            nc.vector.quantize_mx(
-                out=w_codes[:, cols].bitcast(FP8X4),
-                scales=w_scale[:, cols],
-                in_=w_bf[t0 // 2][:, t0 % 2 : t0 % 2 + t1 - t0, :, :].rearrange("p t m j -> p (t m j)"),
-            )
+        def quantize_w(lo, hi, src):
+            nc.vector.quantize_mx(out=w_codes[:, lo:hi].bitcast(FP8X4), scales=w_scale[:, lo:hi], in_=src)
 
-        deal(nc.scalar.copy, 0, 0, slice(0, P))
-        deal(nc.scalar.copy, 1, 0, slice(0, P // 2))
-        deal(nc.scalar.copy, 0, 1, slice(0, P))
-        deal(nc.vector.tensor_copy, 1, 0, slice(P // 2, P))
-        quantize_w(0, 1)
-        deal(nc.vector.tensor_copy, 1, 1, slice(0, P))
-        quantize_w(1, 2)
-        quantize_x(1, "w_raw1")
-        quantize_w(2, 4)
+        def quantize_plain(a):
+            for t in range(2):
+                lo = P * (2 + t) + a * P // 2
+                quantize_w(lo, lo + P // 2, w_plain[:, t, a * P // 2 : (a + 1) * P // 2, :].rearrange("p m j -> p (m j)"))
+
+        w_mixed[0] = keep.tile([P, 2, P // 2, PACK], BF16, name="w_mixed0", tag="w_mixed", align_bytes=64)
+        deal(nc.scalar.copy, w_mixed[0][:], 0, 0)
+        quantize_w(0, P, w_mixed[0][:].rearrange("p t m j -> p (t m j)"))
+        deal(nc.scalar.copy, w_plain[:, :, low, :], 0, 1)
+        w_mixed[1] = keep.tile([P, 2, P // 2, PACK], BF16, name="w_mixed1", tag="w_mixed", align_bytes=64)
+        deal(nc.vector.tensor_copy, w_mixed[1][:], 1, 0)
+        quantize_plain(0)
+        quantize_w(P, 2 * P, w_mixed[1][:].rearrange("p t m j -> p (t m j)"))
 
         pieces = [(t, 0, FIRST) for t in range(2)] + [(t, FIRST, S) for t in range(2)] + [(t, 0, S) for t in range(2, PACK)]
         for t, lo, hi in pieces:
+            if t == 2:
+                deal(nc.scalar.copy, w_plain[:, :, high, :], 1, 1)
+                quantize_plain(1)
             name = "h%d_%d" % (t, lo)
             acc = psum.tile([P, hi - lo], F32, name=name + "_acc", tag="bank")
             cuts = [lo, hi] if hi <= HALF else [lo, HALF, hi]
@@ -155,18 +155,24 @@ def tile_picked_unet_none_e_kernel(tc, xT, w1, w2_words, w2_scales, skip, offs, 
 
         chunks = len(CHUNKS)
         starts = [sum(CHUNKS[:c]) for c in range(chunks + 1)]
-        z_pair = [z[:, 0 : 2 * U].rearrange("p (e v) -> p e v", e=2) for z in (z_low, z_high)]
-        for t in range(PACK - 1):
-            cuts = [0, starts[2], U] if t == 1 else [0, U]
-            for v0, v1 in zip(cuts, cuts[1:]):
-                nc.gpsimd.tensor_tensor(
-                    out=z_pair[t // 2][:, t % 2, v0:v1], in0=up[t][:, v0:v1], in1=skip_plane[t][:, v0:v1], op=ADD
-                )
+        z_late = z_high[:]
+        for a in range(U // PIECE):
+            cells = slice(a * PIECE, (a + 1) * PIECE)
+            nc.gpsimd.tensor_tensor(out=z_low[a][:, 0, :], in0=up[0][:, cells], in1=skip_plane[0][:, cells], op=ADD)
+            nc.sync.dma_start(out=z_low[a][low, 1, :], in_=z_low[a][high, 0, :])
+        for a in range(U // PIECE):
+            cells = slice(a * PIECE, (a + 1) * PIECE)
+            z_mixed = keep.tile([P, PIECE], BF16, name="z_mixed%d" % a)
+            nc.gpsimd.tensor_tensor(out=z_mixed[:], in0=up[1][:, cells], in1=skip_plane[1][:, cells], op=ADD)
+            for e, part in enumerate([low, high]):
+                nc.sync.dma_start(out=z_low[a][high, e, :], in_=z_mixed[part, :])
 
-        z_bf = [keep.tile([P, CHUNKS[c], PACK], BF16, name="z_bf%d" % c, align_bytes=64) for c in range(chunks)]
-        for c in range(chunks):
-            cells = slice(starts[c], starts[c + 1])
-            nc.scalar.copy(out=z_bf[c][:, :, 0:2], in_=z_pair[0][:, :, cells].rearrange("p e v -> p v e"))
+        nc.gpsimd.tensor_tensor(out=z_late[:, 0, :], in0=up[2][:], in1=skip_plane[2], op=ADD)
+
+        z_bf = keep.tile([P, U, PACK], BF16, name="z_bf", align_bytes=64)
+        for a in range(U // PIECE):
+            cells = slice(a * PIECE, (a + 1) * PIECE)
+            nc.scalar.copy(out=z_bf[:, cells, 0:2], in_=z_low[a].rearrange("p e v -> p v e"))
 
         out_rows = out.rearrange("(a p) v -> p a v", p=P)
 
@@ -186,13 +192,13 @@ def tile_picked_unet_none_e_kernel(tc, xT, w1, w2_words, w2_scales, skip, offs, 
         def add_last(c):
             cells = slice(starts[c], starts[c + 1])
             other = skip_first[:] if c == 0 else skip_plane[3][:, cells]
-            nc.vector.tensor_tensor(out=z_pair[1][:, 1, cells], in0=up[3][:, cells], in1=other, op=ADD)
+            nc.vector.tensor_tensor(out=z_late[:, 1, cells], in0=up[3][:, cells], in1=other, op=ADD)
 
         def weave(c):
             cells = slice(starts[c], starts[c + 1])
             on_scalar = c % 2 == 0 and c < SCALAR_WEAVES_BELOW
             copy = nc.scalar.copy if on_scalar else nc.vector.tensor_copy
-            copy(out=z_bf[c][:, :, 2:4], in_=z_pair[1][:, :, cells].rearrange("p e v -> p v e"))
+            copy(out=z_bf[:, cells, 2:4], in_=z_late[:, :, cells].rearrange("p e v -> p v e"))
 
         accs = {}
 
@@ -202,7 +208,7 @@ def tile_picked_unet_none_e_kernel(tc, xT, w1, w2_words, w2_scales, skip, offs, 
             nc.vector.quantize_mx(
                 out=z_codes[:].bitcast(FP8X4),
                 scales=z_scale[:],
-                in_=z_bf[c][:].rearrange("p v t -> p (v t)"),
+                in_=z_bf[:, starts[c] : starts[c + 1], :].rearrange("p v t -> p (v t)"),
             )
             if CHUNKS[c] == NARROW:
                 both = psum.tile([P, N // P, CHUNKS[c]], F32, name="out_acc%d" % c, tag="bank")

@@ -56,7 +56,7 @@ def tile_picked_unet_none_e_kernel(tc, xT, w1, w2_words, w2_scales, skip, offs, 
         skip_rows = skip.rearrange("(p t) v -> p t v", t=PACK)
         z_high = keep.tile([P, 2, U], BF16, name="z_high")
         z_low = [keep.tile([P, 2, PIECE], BF16, name="z_low%d" % a)[:] for a in range(U // PIECE - 1)]
-        z_low.append(z_high[:, 1, :].rearrange("p (e v) -> p e v", e=2)[:, :, NARROW // 2 : NARROW // 2 + PIECE])
+        z_low.insert(U // PIECE - 2, z_high[:, 1, :].rearrange("p (e v) -> p e v", e=2)[:, :, NARROW // 2 : NARROW // 2 + PIECE])
         skip_plane = [keep.tile([P, U], F32, name="skip_plane%d" % t)[:] for t in range(PACK)]
         low, high = slice(0, P // 2), slice(P // 2, P)
         nc.sync.dma_start(out=skip_plane[3], in_=skip_rows[:, 3, :])
@@ -196,7 +196,7 @@ def tile_picked_unet_none_e_kernel(tc, xT, w1, w2_words, w2_scales, skip, offs, 
 
         def weave(c):
             cells = slice(starts[c], starts[c + 1])
-            on_scalar = c % 2 == 0 and c < SCALAR_WEAVES_BELOW
+            on_scalar = c == 2
             copy = nc.scalar.copy if on_scalar else nc.vector.tensor_copy
             copy(out=z_bf[:, cells, 2:4], in_=z_late[:, :, cells].rearrange("p e v -> p v e"))
 

@@ -99,8 +99,8 @@ def tile_picked_unet_none_e_kernel(tc, xT, w1, w2_words, w2_scales, skip, offs, 
 
         def deal(copy, dst, a, b):
             copy(
-                out=dst.rearrange("p t m j -> p m t j"),
-                in_=w_raw[a][:].rearrange("p j (m t) -> p m t j", t=PACK)[:, :, 2 * b : 2 * b + 2, :],
+                out=dst.rearrange("p t m j -> p m j t"),
+                in_=w_raw[a][:].rearrange("p j (m t) -> p m j t", t=PACK)[:, :, :, 2 * b : 2 * b + 2],
             )
 
         def quantize_w(lo, hi, src):

@@ -1,7 +1,6 @@
 from contextlib import ExitStack
 
 import concourse.mybir as mybir
-from concourse.masks import make_identity
 
 K, T, S, H, N, U = 512, 2048, 512, 512, 256, 1024
 FLOPS = 2 * K * H * S + 2 * H * N * U
@@ -15,6 +14,7 @@ U8 = mybir.dt.uint8
 FP8X4 = mybir.dt.float8_e4m3fn_x4
 FP4X4 = mybir.dt.float4_e2m1fn_x4
 ADD = mybir.AluOpType.add
+COPY = mybir.ActivationFunctionType.Copy
 
 P = 128
 PACK = 4
@@ -23,20 +23,19 @@ QUADRANT = 32
 BANKS = 8
 HALF = S // 2
 FIRST = 128
-PIECE = 256
-WARM_UPS = 2
+RUN = 4
+SPLIT = 576
 
 NARROW, WIDE = 128, 256
 CHUNKS = [NARROW, WIDE, WIDE, NARROW, WIDE]
-SCALAR_WEAVES_BELOW = 3
+SCALAR_WEAVES = [1, 3]
 
 
 def tile_picked_unet_none_e_kernel(tc, xT, w1, w2_words, w2_scales, skip, offs, cell, out):
     nc = tc.nc
     with ExitStack() as ctx:
         keep = ctx.enter_context(tc.tile_pool(name="keep", bufs=1))
-        psum = ctx.enter_context(tc.psum_pool(name="psum", bufs=BANKS - 1))
-        held = ctx.enter_context(tc.psum_pool(name="held", bufs=1))
+        psum = ctx.enter_context(tc.psum_pool(name="psum", bufs=BANKS))
 
         offs_sb = keep.tile([P, S // LIST_COL], U16, name="offs_sb")
         cell_sb = keep.tile([P, S // LIST_COL], U16, name="cell_sb")
@@ -54,16 +53,9 @@ def tile_picked_unet_none_e_kernel(tc, xT, w1, w2_words, w2_scales, skip, offs, 
         nc.sync.dma_start(cell_sb[:], cell)
 
         skip_rows = skip.rearrange("(p t) v -> p t v", t=PACK)
-        z_high = keep.tile([P, 2, U], BF16, name="z_high")
-        z_low = [keep.tile([P, 2, PIECE], BF16, name="z_low%d" % a)[:] for a in range(U // PIECE - 1)]
-        z_low.insert(U // PIECE - 2, z_high[:, 1, :].rearrange("p (e v) -> p e v", e=2)[:, :, NARROW // 2 : NARROW // 2 + PIECE])
-        skip_plane = [keep.tile([P, U], F32, name="skip_plane%d" % t)[:] for t in range(PACK)]
-        low, high = slice(0, P // 2), slice(P // 2, P)
-        nc.sync.dma_start(out=skip_plane[3], in_=skip_rows[:, 3, :])
-        for a, rows in enumerate([low, high]):
-            for e, part in enumerate([low, high]):
-                nc.sync.dma_start(out=skip_plane[a][part, :], in_=skip_rows[rows, e, :])
-        nc.sync.dma_start(out=skip_plane[2], in_=skip_rows[:, 2, :])
+        skip_plane = [keep.tile([P, U], F32, name="skip_plane%d" % t) for t in range(PACK)]
+        for t in range(PACK):
+            nc.sync.dma_start(out=skip_plane[t][:], in_=skip_rows[:, t, :])
         w2_codes = keep.tile([P, 2 * N], U8, name="w2_codes", align_bytes=64)
         nc.sync.dma_start(out=w2_codes[:].bitcast(I32), in_=w2_words[0].bitcast(I32))
         w2_scale = keep.tile([P, N], U8, name="w2_scale", align_bytes=64)
@@ -92,39 +84,38 @@ def tile_picked_unet_none_e_kernel(tc, xT, w1, w2_words, w2_scales, skip, offs, 
                 in_=x_bf[a][:].rearrange("p s j -> p (s j)"),
             )
 
-        w_mixed = {}
-        w_plain = keep.tile([P, 2, P, PACK], BF16, name="w_plain", align_bytes=64)
+        w_bf = [keep.tile([P, 2, P, PACK], BF16, name="w_bf%d" % b, align_bytes=64) for b in range(2)]
         w_codes = keep.tile([P, H], U32, name="w_codes", align_bytes=64)
         w_scale = keep.tile([P, H], U8, name="w_scale", align_bytes=64)
 
-        def deal(copy, dst, a, b):
+        def scalar_copy(out, in_):
+            nc.scalar.activation(out=out, in_=in_, func=COPY)
+
+        def deal(copy, a, b):
             copy(
-                out=dst.rearrange("p t m j -> p m j t"),
+                out=w_bf[b][:, :, a * P // 2 : (a + 1) * P // 2, :].rearrange("p t m j -> p m j t"),
                 in_=w_raw[a][:].rearrange("p j (m t) -> p m j t", t=PACK)[:, :, :, 2 * b : 2 * b + 2],
             )
 
-        def quantize_w(lo, hi, src):
-            nc.vector.quantize_mx(out=w_codes[:, lo:hi].bitcast(FP8X4), scales=w_scale[:, lo:hi], in_=src)
+        def quantize_w(t0, t1):
+            b = t0 // 2
+            nc.vector.quantize_mx(
+                out=w_codes[:, P * t0 : P * t1].bitcast(FP8X4),
+                scales=w_scale[:, P * t0 : P * t1],
+                in_=w_bf[b][:, t0 - 2 * b : t1 - 2 * b, :, :].rearrange("p t m j -> p (t m j)"),
+            )
 
-        def quantize_plain(a):
-            for t in range(2):
-                lo = P * (2 + t) + a * P // 2
-                quantize_w(lo, lo + P // 2, w_plain[:, t, a * P // 2 : (a + 1) * P // 2, :].rearrange("p m j -> p (m j)"))
+        deal(scalar_copy, 0, 0)
+        deal(scalar_copy, 0, 1)
+        deal(nc.vector.tensor_copy, 1, 0)
+        deal(scalar_copy, 1, 1)
+        quantize_w(0, 1)
+        quantize_w(1, 2)
+        quantize_w(2, 4)
 
-        w_mixed[0] = keep.tile([P, 2, P // 2, PACK], BF16, name="w_mixed0", tag="w_mixed", align_bytes=64)
-        deal(nc.scalar.copy, w_mixed[0][:], 0, 0)
-        quantize_w(0, P, w_mixed[0][:].rearrange("p t m j -> p (t m j)"))
-        deal(nc.scalar.copy, w_plain[:, :, low, :], 0, 1)
-        w_mixed[1] = keep.tile([P, 2, P // 2, PACK], BF16, name="w_mixed1", tag="w_mixed", align_bytes=64)
-        deal(nc.vector.tensor_copy, w_mixed[1][:], 1, 0)
-        quantize_plain(0)
-        quantize_w(P, 2 * P, w_mixed[1][:].rearrange("p t m j -> p (t m j)"))
+        h = {}
 
-        pieces = [(t, 0, FIRST) for t in range(2)] + [(t, FIRST, S) for t in range(2)] + [(t, 0, S) for t in range(2, PACK)]
-        for t, lo, hi in pieces:
-            if t == 2:
-                deal(nc.scalar.copy, w_plain[:, :, high, :], 1, 1)
-                quantize_plain(1)
+        def product(t, lo, hi):
             name = "h%d_%d" % (t, lo)
             acc = psum.tile([P, hi - lo], F32, name=name + "_acc", tag="bank")
             cuts = [lo, hi] if hi <= HALF else [lo, HALF, hi]
@@ -140,65 +131,46 @@ def tile_picked_unet_none_e_kernel(tc, xT, w1, w2_words, w2_scales, skip, offs, 
                     start=True,
                     stop=True,
                 )
-            h = keep.tile([P, hi - lo], F32, name=name)
-            nc.scalar.copy(out=h[:], in_=acc[:])
-            nc.vector.tensor_copy(up[t][:].indirect(cell_sb[:, lo // LIST_COL : hi // LIST_COL]), h[:])
+            h[t, lo] = keep.tile([P, hi - lo], F32, name=name)
+            nc.scalar.copy(out=h[t, lo][:], in_=acc[:])
 
-        ident = keep.tile([P, P], F32, name="ident")
-        make_identity(nc, ident[:])
-        turned = psum.tile([P, NARROW], F32, name="turned", tag="bank")
-        nc.tensor.transpose(turned[:], skip_plane[3][:, 0:NARROW], ident[:])
-        turned_sb = keep.tile([P, NARROW], F32, name="turned_sb")
-        nc.scalar.copy(out=turned_sb[:], in_=turned[:])
-        skip_first = held.tile([P, NARROW], F32, name="skip_first", tag="held")
-        nc.tensor.transpose(skip_first[:], turned_sb[:], ident[:])
+        def scatter(copy, t, base, lo, hi):
+            copy(out=up[t][:].indirect(cell_sb[:, lo // LIST_COL : hi // LIST_COL]), in_=h[t, base][:, lo - base : hi - base])
+
+        product(0, 0, FIRST)
+        scatter(nc.vector.tensor_copy, 0, 0, 0, FIRST)
+        product(0, FIRST, S)
+        scatter(nc.vector.tensor_copy, 0, FIRST, FIRST, S)
+        for t in range(1, PACK):
+            product(t, 0, S)
+        scatter(nc.vector.tensor_copy, 2, 0, 0, S)
+        scatter(scalar_copy, 1, 0, 0, S - FIRST)
+        scatter(scalar_copy, 3, 0, 0, FIRST)
+        scatter(scalar_copy, 1, 0, S - FIRST, S)
+        scatter(scalar_copy, 3, 0, FIRST, S)
+
+        z = keep.tile([P, PACK, U], BF16, name="z")
+
+        def add(engine, t, cells):
+            engine.tensor_tensor(out=z[:, t, cells], in0=up[t][:, cells], in1=skip_plane[t][:, cells], op=ADD)
+
+        add(nc.gpsimd, 0, slice(0, U))
+        add(nc.gpsimd, 1, slice(SPLIT, U))
+        add(nc.vector, 1, slice(0, SPLIT))
+        add(nc.vector, 2, slice(0, U))
 
         chunks = len(CHUNKS)
         starts = [sum(CHUNKS[:c]) for c in range(chunks + 1)]
-        z_late = z_high[:]
-        for a in range(U // PIECE):
-            cells = slice(a * PIECE, (a + 1) * PIECE)
-            nc.gpsimd.tensor_tensor(out=z_low[a][:, 0, :], in0=up[0][:, cells], in1=skip_plane[0][:, cells], op=ADD)
-            nc.sync.dma_start(out=z_low[a][low, 1, :], in_=z_low[a][high, 0, :])
-        for a in range(U // PIECE):
-            cells = slice(a * PIECE, (a + 1) * PIECE)
-            z_mixed = keep.tile([P, PIECE], BF16, name="z_mixed%d" % a)
-            nc.gpsimd.tensor_tensor(out=z_mixed[:], in0=up[1][:, cells], in1=skip_plane[1][:, cells], op=ADD)
-            for e, part in enumerate([low, high]):
-                nc.sync.dma_start(out=z_low[a][high, e, :], in_=z_mixed[part, :])
-
-        nc.gpsimd.tensor_tensor(out=z_late[:, 0, :], in0=up[2][:], in1=skip_plane[2], op=ADD)
-
         z_bf = keep.tile([P, U, PACK], BF16, name="z_bf", align_bytes=64)
-        for a in range(U // PIECE):
-            cells = slice(a * PIECE, (a + 1) * PIECE)
-            nc.scalar.copy(out=z_bf[:, cells, 0:2], in_=z_low[a].rearrange("p e v -> p v e"))
-
         out_rows = out.rearrange("(a p) v -> p a v", p=P)
-
-        def warm_up():
-            warm = held.tile([P, H], F32, name="warm", tag="held")
-            for a in range(WARM_UPS):
-                nc.tensor.matmul_mx(
-                    out=warm[:],
-                    lhsT=x_codes[a][:, 0:P].bitcast(FP8X4),
-                    lhsT_scale=x_scale[a][:, 0:P],
-                    rhs=w_codes[:].bitcast(FP8X4),
-                    rhs_scale=w_scale[:],
-                    start=True,
-                    stop=True,
-                )
-
-        def add_last(c):
-            cells = slice(starts[c], starts[c + 1])
-            other = skip_first[:] if c == 0 else skip_plane[3][:, cells]
-            nc.vector.tensor_tensor(out=z_late[:, 1, cells], in0=up[3][:, cells], in1=other, op=ADD)
 
         def weave(c):
             cells = slice(starts[c], starts[c + 1])
-            on_scalar = c == 2
-            copy = nc.scalar.copy if on_scalar else nc.vector.tensor_copy
-            copy(out=z_bf[:, cells, 2:4], in_=z_late[:, :, cells].rearrange("p e v -> p v e"))
+            copy = nc.scalar.copy if c in SCALAR_WEAVES else nc.vector.tensor_copy
+            copy(
+                out=z_bf[:, cells, :].rearrange("p (c i) t -> p c t i", i=RUN),
+                in_=z[:, :, cells].rearrange("p t (c i) -> p c t i", i=RUN),
+            )
 
         accs = {}
 
@@ -240,8 +212,10 @@ def tile_picked_unet_none_e_kernel(tc, xT, w1, w2_words, w2_scales, skip, offs, 
                 copy(out=res[:, rows, :], in_=acc)
                 nc.sync.dma_start(out=out_rows[:, rows, cells], in_=res[:, rows, :])
 
+        def add_last(c):
+            add(nc.vector, 3, slice(starts[c], starts[c + 1]))
+
         add_last(0)
-        warm_up()
         add_last(1)
         weave(0)
         for c in range(chunks):

@@ -24,7 +24,6 @@ BANKS = 8
 HALF = S // 2
 FIRST = 128
 RUN = 4
-SPLIT = 576
 
 NARROW, WIDE = 128, 256
 CHUNKS = [NARROW, WIDE, WIDE, NARROW, WIDE]
@@ -70,11 +69,16 @@ def tile_picked_unet_none_e_kernel(tc, xT, w1, w2_words, w2_scales, skip, offs, 
         for t in range(PACK):
             nc.vector.memset(up[t][:], 0.0)
 
+        def scalar_copy(out, in_):
+            nc.scalar.activation(out=out, in_=in_, func=COPY)
+
         x_bf = [keep.tile([P, HALF, PACK], BF16, name="x_bf%d" % a, align_bytes=64) for a in range(2)]
+        x_pair = [keep.tile([P, 2, HALF], BF16, name="x_pair%d" % e) for e in range(2)]
         for j in range(PACK):
-            for a in range(2):
-                cols = slice(a * HALF // LIST_COL, (a + 1) * HALF // LIST_COL)
-                nc.vector.tensor_copy(x_bf[a][:, :, j], x_plane[j][:].indirect(offs_sb[:, cols]))
+            nc.vector.tensor_copy(x_bf[0][:, :, j], x_plane[j][:].indirect(offs_sb[:, 0 : HALF // LIST_COL]))
+            scalar_copy(out=x_pair[j // 2][:, j % 2, :], in_=x_plane[j][:].indirect(offs_sb[:, HALF // LIST_COL :]))
+            if j % 2:
+                nc.vector.tensor_copy(x_bf[1][:, :, j - 1 : j + 1], x_pair[j // 2][:].rearrange("p e s -> p s e"))
         x_codes = [keep.tile([P, HALF], U32, name="x_codes%d" % a, align_bytes=64) for a in range(2)]
         x_scale = [keep.tile([P, HALF], U8, name="x_scale%d" % a, align_bytes=64) for a in range(2)]
         for a in range(2):
@@ -87,9 +91,6 @@ def tile_picked_unet_none_e_kernel(tc, xT, w1, w2_words, w2_scales, skip, offs, 
         w_bf = [keep.tile([P, 2, P, PACK], BF16, name="w_bf%d" % b, align_bytes=64) for b in range(2)]
         w_codes = keep.tile([P, H], U32, name="w_codes", align_bytes=64)
         w_scale = keep.tile([P, H], U8, name="w_scale", align_bytes=64)
-
-        def scalar_copy(out, in_):
-            nc.scalar.activation(out=out, in_=in_, func=COPY)
 
         def deal(copy, a, b):
             copy(
@@ -118,7 +119,7 @@ def tile_picked_unet_none_e_kernel(tc, xT, w1, w2_words, w2_scales, skip, offs, 
         def product(t, lo, hi):
             name = "h%d_%d" % (t, lo)
             acc = psum.tile([P, hi - lo], F32, name=name + "_acc", tag="bank")
-            cuts = [lo, hi] if hi <= HALF else [lo, HALF, hi]
+            cuts = [lo, HALF, hi] if lo < HALF < hi else [lo, hi]
             for c0, c1 in zip(cuts, cuts[1:]):
                 a = c0 // HALF
                 cols = slice(c0 - a * HALF, c1 - a * HALF)
@@ -155,8 +156,7 @@ def tile_picked_unet_none_e_kernel(tc, xT, w1, w2_words, w2_scales, skip, offs, 
             engine.tensor_tensor(out=z[:, t, cells], in0=up[t][:, cells], in1=skip_plane[t][:, cells], op=ADD)
 
         add(nc.gpsimd, 0, slice(0, U))
-        add(nc.gpsimd, 1, slice(SPLIT, U))
-        add(nc.vector, 1, slice(0, SPLIT))
+        add(nc.vector, 1, slice(0, U))
         add(nc.vector, 2, slice(0, U))
 
         chunks = len(CHUNKS)

@@ -28,6 +28,8 @@ RUN = 4
 NARROW, WIDE = 128, 256
 CHUNKS = [NARROW, WIDE, WIDE, NARROW, WIDE]
 SCALAR_WEAVES = [1, 3]
+DEAL_CUT = 104
+EARLY = 768
 
 
 def tile_picked_unet_none_e_kernel(tc, xT, w1, w2_words, w2_scales, skip, offs, cell, out):
@@ -52,8 +54,11 @@ def tile_picked_unet_none_e_kernel(tc, xT, w1, w2_words, w2_scales, skip, offs, 
         nc.sync.dma_start(cell_sb[:], cell)
 
         skip_rows = skip.rearrange("(p t) v -> p t v", t=PACK)
+        skip_first = keep.tile([P, EARLY], F32, name="skip_first", tag="shared")
+        nc.sync.dma_start(out=skip_first[:], in_=skip_rows[:, 0, 0:EARLY])
         skip_plane = [keep.tile([P, U], F32, name="skip_plane%d" % t) for t in range(PACK)]
-        for t in range(PACK):
+        nc.sync.dma_start(out=skip_plane[0][:, EARLY:], in_=skip_rows[:, 0, EARLY:])
+        for t in range(1, PACK):
             nc.sync.dma_start(out=skip_plane[t][:], in_=skip_rows[:, t, :])
         w2_codes = keep.tile([P, 2 * N], U8, name="w2_codes", align_bytes=64)
         nc.sync.dma_start(out=w2_codes[:].bitcast(I32), in_=w2_words[0].bitcast(I32))
@@ -88,28 +93,27 @@ def tile_picked_unet_none_e_kernel(tc, xT, w1, w2_words, w2_scales, skip, offs, 
                 in_=x_bf[a][:].rearrange("p s j -> p (s j)"),
             )
 
-        w_bf = [keep.tile([P, 2, P, PACK], BF16, name="w_bf%d" % b, align_bytes=64) for b in range(2)]
+        w_bf = keep.tile([P, PACK, P, PACK], BF16, name="w_bf", align_bytes=64)
         w_codes = keep.tile([P, H], U32, name="w_codes", align_bytes=64)
         w_scale = keep.tile([P, H], U8, name="w_scale", align_bytes=64)
 
-        def deal(copy, a, b):
+        def deal(copy, lo, hi):
+            a = lo // (P // 2)
             copy(
-                out=w_bf[b][:, :, a * P // 2 : (a + 1) * P // 2, :].rearrange("p t m j -> p m j t"),
-                in_=w_raw[a][:].rearrange("p j (m t) -> p m j t", t=PACK)[:, :, :, 2 * b : 2 * b + 2],
+                out=w_bf[:, :, lo:hi, :].rearrange("p t m j -> p m j t"),
+                in_=w_raw[a][:].rearrange("p j (m t) -> p m j t", t=PACK)[:, lo - a * P // 2 : hi - a * P // 2, :, :],
             )
 
         def quantize_w(t0, t1):
-            b = t0 // 2
             nc.vector.quantize_mx(
                 out=w_codes[:, P * t0 : P * t1].bitcast(FP8X4),
                 scales=w_scale[:, P * t0 : P * t1],
-                in_=w_bf[b][:, t0 - 2 * b : t1 - 2 * b, :, :].rearrange("p t m j -> p (t m j)"),
+                in_=w_bf[:, t0:t1, :, :].rearrange("p t m j -> p (t m j)"),
             )
 
-        deal(scalar_copy, 0, 0)
-        deal(scalar_copy, 0, 1)
-        deal(nc.vector.tensor_copy, 1, 0)
-        deal(scalar_copy, 1, 1)
+        deal(scalar_copy, 0, P // 2)
+        deal(nc.vector.tensor_copy, P // 2, DEAL_CUT)
+        deal(scalar_copy, DEAL_CUT, P)
         quantize_w(0, 1)
         quantize_w(1, 2)
         quantize_w(2, 4)
@@ -150,26 +154,28 @@ def tile_picked_unet_none_e_kernel(tc, xT, w1, w2_words, w2_scales, skip, offs, 
         scatter(scalar_copy, 1, 0, S - FIRST, S)
         scatter(scalar_copy, 3, 0, FIRST, S)
 
-        z = keep.tile([P, PACK, U], BF16, name="z")
+        z_bf = keep.tile([P, U, PACK], BF16, name="z_bf", align_bytes=64)
+        nc.gpsimd.tensor_tensor(out=z_bf[:, 0:EARLY, 0], in0=up[0][:, 0:EARLY], in1=skip_first[:], op=ADD)
+        z = keep.tile([P, PACK, U], BF16, name="z", tag="shared")
 
         def add(engine, t, cells):
             engine.tensor_tensor(out=z[:, t, cells], in0=up[t][:, cells], in1=skip_plane[t][:, cells], op=ADD)
 
-        add(nc.gpsimd, 0, slice(0, U))
+        add(nc.vector, 0, slice(EARLY, U))
         add(nc.vector, 1, slice(0, U))
         add(nc.vector, 2, slice(0, U))
 
         chunks = len(CHUNKS)
         starts = [sum(CHUNKS[:c]) for c in range(chunks + 1)]
-        z_bf = keep.tile([P, U, PACK], BF16, name="z_bf", align_bytes=64)
         out_rows = out.rearrange("(a p) v -> p a v", p=P)
 
         def weave(c):
             cells = slice(starts[c], starts[c + 1])
             copy = nc.scalar.copy if c in SCALAR_WEAVES else nc.vector.tensor_copy
+            t0 = 1 if starts[c] < EARLY else 0
             copy(
-                out=z_bf[:, cells, :].rearrange("p (c i) t -> p c t i", i=RUN),
-                in_=z[:, :, cells].rearrange("p t (c i) -> p c t i", i=RUN),
+                out=z_bf[:, cells, t0:].rearrange("p (c i) t -> p c t i", i=RUN),
+                in_=z[:, t0:, cells].rearrange("p t (c i) -> p c t i", i=RUN),
             )
 
         accs = {}

@@ -26,10 +26,9 @@ FIRST = 128
 RUN = 4
 
 NARROW, WIDE = 128, 256
-CHUNKS = [NARROW, WIDE, WIDE, NARROW, WIDE]
+CHUNKS = [NARROW, WIDE, NARROW, WIDE, WIDE]
 SCALAR_WEAVES = [1, 3]
 DEAL_CUT = 104
-EARLY = 768
 
 
 def tile_picked_unet_none_e_kernel(tc, xT, w1, w2_words, w2_scales, skip, offs, cell, out):
@@ -54,10 +53,10 @@ def tile_picked_unet_none_e_kernel(tc, xT, w1, w2_words, w2_scales, skip, offs, 
         nc.sync.dma_start(cell_sb[:], cell)
 
         skip_rows = skip.rearrange("(p t) v -> p t v", t=PACK)
-        skip_first = keep.tile([P, EARLY], F32, name="skip_first", tag="shared")
-        nc.sync.dma_start(out=skip_first[:], in_=skip_rows[:, 0, 0:EARLY])
+        skip_first = keep.tile([P, U - NARROW], F32, name="skip_first", tag="shared")
+        nc.sync.dma_start(out=skip_first[:], in_=skip_rows[:, 0, NARROW:])
         skip_plane = [keep.tile([P, U], F32, name="skip_plane%d" % t) for t in range(PACK)]
-        nc.sync.dma_start(out=skip_plane[0][:, EARLY:], in_=skip_rows[:, 0, EARLY:])
+        nc.sync.dma_start(out=skip_plane[0][:, 0:NARROW], in_=skip_rows[:, 0, 0:NARROW])
         for t in range(1, PACK):
             nc.sync.dma_start(out=skip_plane[t][:], in_=skip_rows[:, t, :])
         w2_codes = keep.tile([P, 2 * N], U8, name="w2_codes", align_bytes=64)
@@ -155,15 +154,15 @@ def tile_picked_unet_none_e_kernel(tc, xT, w1, w2_words, w2_scales, skip, offs, 
         scatter(scalar_copy, 3, 0, FIRST, S)
 
         z_bf = keep.tile([P, U, PACK], BF16, name="z_bf", align_bytes=64)
-        nc.gpsimd.tensor_tensor(out=z_bf[:, 0:EARLY, 0], in0=up[0][:, 0:EARLY], in1=skip_first[:], op=ADD)
+        nc.gpsimd.tensor_tensor(out=z_bf[:, NARROW:, 0], in0=up[0][:, NARROW:], in1=skip_first[:], op=ADD)
         z = keep.tile([P, PACK, U], BF16, name="z", tag="shared")
 
         def add(engine, t, cells):
             engine.tensor_tensor(out=z[:, t, cells], in0=up[t][:, cells], in1=skip_plane[t][:, cells], op=ADD)
 
-        add(nc.vector, 0, slice(EARLY, U))
+        add(nc.vector, 0, slice(0, NARROW))
         add(nc.vector, 1, slice(0, U))
-        add(nc.vector, 2, slice(0, U))
+        add(nc.vector, 2, slice(0, NARROW + WIDE))
 
         chunks = len(CHUNKS)
         starts = [sum(CHUNKS[:c]) for c in range(chunks + 1)]
@@ -172,7 +171,7 @@ def tile_picked_unet_none_e_kernel(tc, xT, w1, w2_words, w2_scales, skip, offs, 
         def weave(c):
             cells = slice(starts[c], starts[c + 1])
             copy = nc.scalar.copy if c in SCALAR_WEAVES else nc.vector.tensor_copy
-            t0 = 1 if starts[c] < EARLY else 0
+            t0 = 1 if c > 0 else 0
             copy(
                 out=z_bf[:, cells, t0:].rearrange("p (c i) t -> p c t i", i=RUN),
                 in_=z[:, t0:, cells].rearrange("p t (c i) -> p c t i", i=RUN),
@@ -219,7 +218,8 @@ def tile_picked_unet_none_e_kernel(tc, xT, w1, w2_words, w2_scales, skip, offs, 
                 nc.sync.dma_start(out=out_rows[:, rows, cells], in_=res[:, rows, :])
 
         def add_last(c):
-            add(nc.vector, 3, slice(starts[c], starts[c + 1]))
+            for t in range(2 if c >= 2 else 3, PACK):
+                add(nc.vector, t, slice(starts[c], starts[c + 1]))
 
         add_last(0)
         add_last(1)

@@ -22,13 +22,12 @@ LIST_COL = 16
 QUADRANT = 32
 BANKS = 8
 HALF = S // 2
-FIRST = 128
+SHORT = 128
 RUN = 4
+DEAL_CUT = 104
 
 NARROW, WIDE = 128, 256
-CHUNKS = [NARROW, WIDE, NARROW, WIDE, WIDE]
-SCALAR_WEAVES = [1, 3]
-DEAL_CUT = 104
+CHUNKS = [NARROW, WIDE, WIDE, WIDE, NARROW]
 
 
 def tile_picked_unet_none_e_kernel(tc, xT, w1, w2_words, w2_scales, skip, offs, cell, out):
@@ -53,10 +52,12 @@ def tile_picked_unet_none_e_kernel(tc, xT, w1, w2_words, w2_scales, skip, offs, 
         nc.sync.dma_start(cell_sb[:], cell)
 
         skip_rows = skip.rearrange("(p t) v -> p t v", t=PACK)
-        skip_first = keep.tile([P, U - NARROW], F32, name="skip_first", tag="shared")
-        nc.sync.dma_start(out=skip_first[:], in_=skip_rows[:, 0, NARROW:])
+        wide_cells = slice(NARROW, U - NARROW)
+        skip_wide = keep.tile([P, U - 2 * NARROW], F32, name="skip_wide", tag="skip_then_z")
+        nc.sync.dma_start(out=skip_wide[:], in_=skip_rows[:, 0, wide_cells])
         skip_plane = [keep.tile([P, U], F32, name="skip_plane%d" % t) for t in range(PACK)]
-        nc.sync.dma_start(out=skip_plane[0][:, 0:NARROW], in_=skip_rows[:, 0, 0:NARROW])
+        for narrow_cells in (slice(0, NARROW), slice(U - NARROW, U)):
+            nc.sync.dma_start(out=skip_plane[0][:, narrow_cells], in_=skip_rows[:, 0, narrow_cells])
         for t in range(1, PACK):
             nc.sync.dma_start(out=skip_plane[t][:], in_=skip_rows[:, t, :])
         w2_codes = keep.tile([P, 2 * N], U8, name="w2_codes", align_bytes=64)
@@ -83,12 +84,13 @@ def tile_picked_unet_none_e_kernel(tc, xT, w1, w2_words, w2_scales, skip, offs, 
             scalar_copy(out=x_pair[j // 2][:, j % 2, :], in_=x_plane[j][:].indirect(offs_sb[:, HALF // LIST_COL :]))
             if j % 2:
                 nc.vector.tensor_copy(x_bf[1][:, :, j - 1 : j + 1], x_pair[j // 2][:].rearrange("p e s -> p s e"))
-        x_codes = [keep.tile([P, HALF], U32, name="x_codes%d" % a, align_bytes=64) for a in range(2)]
-        x_scale = [keep.tile([P, HALF], U8, name="x_scale%d" % a, align_bytes=64) for a in range(2)]
+        x_codes = keep.tile([P, S], U32, name="x_codes", align_bytes=64)
+        x_scale = keep.tile([P, S], U8, name="x_scale", align_bytes=64)
         for a in range(2):
+            points = slice(a * HALF, (a + 1) * HALF)
             nc.vector.quantize_mx(
-                out=x_codes[a][:].bitcast(FP8X4),
-                scales=x_scale[a][:],
+                out=x_codes[:, points].bitcast(FP8X4),
+                scales=x_scale[:, points],
                 in_=x_bf[a][:].rearrange("p s j -> p (s j)"),
             )
 
@@ -103,78 +105,71 @@ def tile_picked_unet_none_e_kernel(tc, xT, w1, w2_words, w2_scales, skip, offs, 
                 in_=w_raw[a][:].rearrange("p j (m t) -> p m j t", t=PACK)[:, lo - a * P // 2 : hi - a * P // 2, :, :],
             )
 
-        def quantize_w(t0, t1):
+        deal(scalar_copy, 0, P // 2)
+        deal(nc.vector.tensor_copy, P // 2, DEAL_CUT)
+        deal(scalar_copy, DEAL_CUT, P)
+        for t0, t1 in [(0, 1), (1, 2), (2, PACK)]:
             nc.vector.quantize_mx(
                 out=w_codes[:, P * t0 : P * t1].bitcast(FP8X4),
                 scales=w_scale[:, P * t0 : P * t1],
                 in_=w_bf[:, t0:t1, :, :].rearrange("p t m j -> p (t m j)"),
             )
 
-        deal(scalar_copy, 0, P // 2)
-        deal(nc.vector.tensor_copy, P // 2, DEAL_CUT)
-        deal(scalar_copy, DEAL_CUT, P)
-        quantize_w(0, 1)
-        quantize_w(1, 2)
-        quantize_w(2, 4)
-
-        h = {}
-
-        def product(t, lo, hi):
+        def product(t, cuts):
+            lo, hi = cuts[0], cuts[-1]
             name = "h%d_%d" % (t, lo)
             acc = psum.tile([P, hi - lo], F32, name=name + "_acc", tag="bank")
-            cuts = [lo, HALF, hi] if lo < HALF < hi else [lo, hi]
             for c0, c1 in zip(cuts, cuts[1:]):
-                a = c0 // HALF
-                cols = slice(c0 - a * HALF, c1 - a * HALF)
                 nc.tensor.matmul_mx(
                     out=acc[:, c0 - lo : c1 - lo],
                     lhsT=w_codes[:, P * t : P * (t + 1)].bitcast(FP8X4),
                     lhsT_scale=w_scale[:, P * t : P * (t + 1)],
-                    rhs=x_codes[a][:, cols].bitcast(FP8X4),
-                    rhs_scale=x_scale[a][:, cols],
+                    rhs=x_codes[:, c0:c1].bitcast(FP8X4),
+                    rhs_scale=x_scale[:, c0:c1],
                     start=True,
                     stop=True,
                 )
-            h[t, lo] = keep.tile([P, hi - lo], F32, name=name)
-            nc.scalar.copy(out=h[t, lo][:], in_=acc[:])
+            h = keep.tile([P, hi - lo], F32, name=name)
+            nc.scalar.copy(out=h[:], in_=acc[:])
+            return h
 
-        def scatter(copy, t, base, lo, hi):
-            copy(out=up[t][:].indirect(cell_sb[:, lo // LIST_COL : hi // LIST_COL]), in_=h[t, base][:, lo - base : hi - base])
+        def scatter(copy, t, lo, hi, values):
+            copy(out=up[t][:].indirect(cell_sb[:, lo // LIST_COL : hi // LIST_COL]), in_=values)
 
-        product(0, 0, FIRST)
-        scatter(nc.vector.tensor_copy, 0, 0, 0, FIRST)
-        product(0, FIRST, S)
-        scatter(nc.vector.tensor_copy, 0, FIRST, FIRST, S)
-        for t in range(1, PACK):
-            product(t, 0, S)
-        scatter(nc.vector.tensor_copy, 2, 0, 0, S)
-        scatter(scalar_copy, 1, 0, 0, S - FIRST)
-        scatter(scalar_copy, 3, 0, 0, FIRST)
-        scatter(scalar_copy, 1, 0, S - FIRST, S)
-        scatter(scalar_copy, 3, 0, FIRST, S)
+        scatter(nc.vector.tensor_copy, 0, 0, SHORT, product(0, [0, SHORT])[:])
+        scatter(nc.vector.tensor_copy, 0, SHORT, S, product(0, [SHORT, HALF, S])[:])
+        h1, h2, h3 = [product(t, [0, S]) for t in range(1, PACK)]
+        scatter(nc.vector.tensor_copy, 2, 0, S, h2[:])
+        for t, values, lo, hi in [(1, h1, 0, S - SHORT), (3, h3, 0, SHORT), (1, h1, S - SHORT, S), (3, h3, SHORT, S)]:
+            scatter(scalar_copy, t, lo, hi, values[:, lo:hi])
 
         z_bf = keep.tile([P, U, PACK], BF16, name="z_bf", align_bytes=64)
-        nc.gpsimd.tensor_tensor(out=z_bf[:, NARROW:, 0], in0=up[0][:, NARROW:], in1=skip_first[:], op=ADD)
-        z = keep.tile([P, PACK, U], BF16, name="z", tag="shared")
-
-        def add(engine, t, cells):
-            engine.tensor_tensor(out=z[:, t, cells], in0=up[t][:, cells], in1=skip_plane[t][:, cells], op=ADD)
-
-        add(nc.vector, 0, slice(0, NARROW))
-        add(nc.vector, 1, slice(0, U))
-        add(nc.vector, 2, slice(0, NARROW + WIDE))
+        nc.gpsimd.tensor_tensor(out=z_bf[:, wide_cells, 0], in0=up[0][:, wide_cells], in1=skip_wide[:], op=ADD)
+        z = keep.tile([P, PACK, U], BF16, name="z", tag="skip_then_z")
 
         chunks = len(CHUNKS)
         starts = [sum(CHUNKS[:c]) for c in range(chunks + 1)]
+        chunk_cells = [slice(starts[c], starts[c + 1]) for c in range(chunks)]
         out_rows = out.rearrange("(a p) v -> p a v", p=P)
 
+        def add(t, cells):
+            nc.vector.tensor_tensor(out=z[:, t, cells], in0=up[t][:, cells], in1=skip_plane[t][:, cells], op=ADD)
+
+        add(0, chunk_cells[0])
+        add(1, slice(0, U))
+        add(2, slice(0, U))
+
+        def add_last(c):
+            add(3, chunk_cells[c])
+            if c == chunks - 1:
+                add(0, chunk_cells[c])
+
         def weave(c):
-            cells = slice(starts[c], starts[c + 1])
-            copy = nc.scalar.copy if c in SCALAR_WEAVES else nc.vector.tensor_copy
-            t0 = 1 if c > 0 else 0
+            copy = nc.scalar.copy if c % 2 else nc.vector.tensor_copy
+            t0 = 1 if CHUNKS[c] == WIDE else 0
             copy(
-                out=z_bf[:, cells, t0:].rearrange("p (c i) t -> p c t i", i=RUN),
-                in_=z[:, t0:, cells].rearrange("p t (c i) -> p c t i", i=RUN),
+                out=z_bf[:, chunk_cells[c], t0:].rearrange("p (c i) t -> p c t i", i=RUN),
+                in_=z[:, t0:, chunk_cells[c]].rearrange("p t (c i) -> p c t i", i=RUN),
             )
 
         accs = {}
@@ -185,9 +180,9 @@ def tile_picked_unet_none_e_kernel(tc, xT, w1, w2_words, w2_scales, skip, offs, 
             nc.vector.quantize_mx(
                 out=z_codes[:].bitcast(FP8X4),
                 scales=z_scale[:],
-                in_=z_bf[:, starts[c] : starts[c + 1], :].rearrange("p v t -> p (v t)"),
+                in_=z_bf[:, chunk_cells[c], :].rearrange("p v t -> p (v t)"),
             )
-            if CHUNKS[c] == NARROW:
+            if c == 0:
                 both = psum.tile([P, N // P, CHUNKS[c]], F32, name="out_acc%d" % c, tag="bank")
                 accs[c] = [both[:]]
                 blocks = [both[:, a, :] for a in range(N // P)]
@@ -209,20 +204,15 @@ def tile_picked_unet_none_e_kernel(tc, xT, w1, w2_words, w2_scales, skip, offs, 
                 )
 
         def store(c):
-            cells = slice(starts[c], starts[c + 1])
             res = keep.tile([P, N // P, CHUNKS[c]], F32, name="res%d" % c)
             for a, acc in enumerate(accs[c]):
                 rows = slice(a, a + acc.shape[1])
                 copy = nc.vector.tensor_copy if (c, a) == (chunks - 1, N // P - 1) else nc.scalar.copy
                 copy(out=res[:, rows, :], in_=acc)
-                nc.sync.dma_start(out=out_rows[:, rows, cells], in_=res[:, rows, :])
+                nc.sync.dma_start(out=out_rows[:, rows, chunk_cells[c]], in_=res[:, rows, :])
 
-        def add_last(c):
-            for t in range(2 if c >= 2 else 3, PACK):
-                add(nc.vector, t, slice(starts[c], starts[c + 1]))
-
-        add_last(0)
         add_last(1)
+        add_last(0)
         weave(0)
         for c in range(chunks):
             if c + 2 < chunks:

@@ -27,7 +27,8 @@ RUN = 4
 DEAL_CUT = 104
 
 NARROW, WIDE = 128, 256
-CHUNKS = [NARROW, WIDE, WIDE, WIDE, NARROW]
+CHUNKS = [NARROW, WIDE, WIDE, NARROW, WIDE]
+EARLY = U - WIDE
 
 
 def tile_picked_unet_none_e_kernel(tc, xT, w1, w2_words, w2_scales, skip, offs, cell, out):
@@ -52,12 +53,10 @@ def tile_picked_unet_none_e_kernel(tc, xT, w1, w2_words, w2_scales, skip, offs, 
         nc.sync.dma_start(cell_sb[:], cell)
 
         skip_rows = skip.rearrange("(p t) v -> p t v", t=PACK)
-        wide_cells = slice(NARROW, U - NARROW)
-        skip_wide = keep.tile([P, U - 2 * NARROW], F32, name="skip_wide", tag="skip_then_z")
-        nc.sync.dma_start(out=skip_wide[:], in_=skip_rows[:, 0, wide_cells])
+        skip_early = keep.tile([P, EARLY], F32, name="skip_early", tag="skip_then_z")
+        nc.sync.dma_start(out=skip_early[:], in_=skip_rows[:, 0, 0:EARLY])
         skip_plane = [keep.tile([P, U], F32, name="skip_plane%d" % t) for t in range(PACK)]
-        for narrow_cells in (slice(0, NARROW), slice(U - NARROW, U)):
-            nc.sync.dma_start(out=skip_plane[0][:, narrow_cells], in_=skip_rows[:, 0, narrow_cells])
+        nc.sync.dma_start(out=skip_plane[0][:, EARLY:], in_=skip_rows[:, 0, EARLY:])
         for t in range(1, PACK):
             nc.sync.dma_start(out=skip_plane[t][:], in_=skip_rows[:, t, :])
         w2_codes = keep.tile([P, 2 * N], U8, name="w2_codes", align_bytes=64)
@@ -144,7 +143,7 @@ def tile_picked_unet_none_e_kernel(tc, xT, w1, w2_words, w2_scales, skip, offs, 
             scatter(scalar_copy, t, lo, hi, values[:, lo:hi])
 
         z_bf = keep.tile([P, U, PACK], BF16, name="z_bf", align_bytes=64)
-        nc.gpsimd.tensor_tensor(out=z_bf[:, wide_cells, 0], in0=up[0][:, wide_cells], in1=skip_wide[:], op=ADD)
+        nc.gpsimd.tensor_tensor(out=z_bf[:, 0:EARLY, 0], in0=up[0][:, 0:EARLY], in1=skip_early[:], op=ADD)
         z = keep.tile([P, PACK, U], BF16, name="z", tag="skip_then_z")
 
         chunks = len(CHUNKS)
@@ -155,18 +154,19 @@ def tile_picked_unet_none_e_kernel(tc, xT, w1, w2_words, w2_scales, skip, offs, 
         def add(t, cells):
             nc.vector.tensor_tensor(out=z[:, t, cells], in0=up[t][:, cells], in1=skip_plane[t][:, cells], op=ADD)
 
-        add(0, chunk_cells[0])
         add(1, slice(0, U))
-        add(2, slice(0, U))
+        add(2, slice(0, starts[2]))
 
         def add_last(c):
             add(3, chunk_cells[c])
-            if c == chunks - 1:
+            if c >= 2:
+                add(2, chunk_cells[c])
+            if starts[c] >= EARLY:
                 add(0, chunk_cells[c])
 
         def weave(c):
             copy = nc.scalar.copy if c % 2 else nc.vector.tensor_copy
-            t0 = 1 if CHUNKS[c] == WIDE else 0
+            t0 = 1 if starts[c] < EARLY else 0
             copy(
                 out=z_bf[:, chunk_cells[c], t0:].rearrange("p (c i) t -> p c t i", i=RUN),
                 in_=z[:, t0:, chunk_cells[c]].rearrange("p t (c i) -> p c t i", i=RUN),
@@ -182,7 +182,7 @@ def tile_picked_unet_none_e_kernel(tc, xT, w1, w2_words, w2_scales, skip, offs, 
                 scales=z_scale[:],
                 in_=z_bf[:, chunk_cells[c], :].rearrange("p v t -> p (v t)"),
             )
-            if c == 0:
+            if CHUNKS[c] == NARROW:
                 both = psum.tile([P, N // P, CHUNKS[c]], F32, name="out_acc%d" % c, tag="bank")
                 accs[c] = [both[:]]
                 blocks = [both[:, a, :] for a in range(N // P)]
@@ -211,8 +211,8 @@ def tile_picked_unet_none_e_kernel(tc, xT, w1, w2_words, w2_scales, skip, offs, 
                 copy(out=res[:, rows, :], in_=acc)
                 nc.sync.dma_start(out=out_rows[:, rows, chunk_cells[c]], in_=res[:, rows, :])
 
-        add_last(1)
         add_last(0)
+        add_last(1)
         weave(0)
         for c in range(chunks):
             if c + 2 < chunks:

@@ -1,6 +1,7 @@
 from contextlib import ExitStack
 
 import concourse.mybir as mybir
+from concourse.masks import make_identity
 
 K, T, S, H, N, U = 512, 2048, 512, 512, 256, 1024
 FLOPS = 2 * K * H * S + 2 * H * N * U
@@ -26,9 +27,9 @@ SHORT = 128
 RUN = 4
 DEAL_CUT = 104
 
-NARROW, WIDE = 128, 256
-CHUNKS = [NARROW, WIDE, WIDE, NARROW, WIDE]
-EARLY = U - WIDE
+EARLY = 768
+TURNED = (U - EARLY) // P
+CHUNKS = [(0, 128), (128, 256), (384, 256), (640, 128)]
 
 
 def tile_picked_unet_none_e_kernel(tc, xT, w1, w2_words, w2_scales, skip, offs, cell, out):
@@ -52,13 +53,6 @@ def tile_picked_unet_none_e_kernel(tc, xT, w1, w2_words, w2_scales, skip, offs, 
             nc.sync.dma_start(out=w_raw[a][:], in_=w_rows[:, :, a * H // 2 : (a + 1) * H // 2])
         nc.sync.dma_start(cell_sb[:], cell)
 
-        skip_rows = skip.rearrange("(p t) v -> p t v", t=PACK)
-        skip_early = keep.tile([P, EARLY], F32, name="skip_early", tag="skip_then_z")
-        nc.sync.dma_start(out=skip_early[:], in_=skip_rows[:, 0, 0:EARLY])
-        skip_plane = [keep.tile([P, U], F32, name="skip_plane%d" % t) for t in range(PACK)]
-        nc.sync.dma_start(out=skip_plane[0][:, EARLY:], in_=skip_rows[:, 0, EARLY:])
-        for t in range(1, PACK):
-            nc.sync.dma_start(out=skip_plane[t][:], in_=skip_rows[:, t, :])
         w2_codes = keep.tile([P, 2 * N], U8, name="w2_codes", align_bytes=64)
         nc.sync.dma_start(out=w2_codes[:].bitcast(I32), in_=w2_words[0].bitcast(I32))
         w2_scale = keep.tile([P, N], U8, name="w2_scale", align_bytes=64)
@@ -68,6 +62,15 @@ def tile_picked_unet_none_e_kernel(tc, xT, w1, w2_words, w2_scales, skip, offs, 
                 out=w2_scale[QUADRANT * q : QUADRANT * q + 4, :].bitcast(I32),
                 in_=w2_scales[0, 4 * q : 4 * q + 4, :].bitcast(I32),
             )
+
+        skip_rows = skip.rearrange("(p t) v -> p t v", t=PACK)
+        skip_late = keep.tile([P, PACK, U - EARLY], F32, name="skip_late")
+        nc.sync.dma_start(out=skip_late[:], in_=skip_rows[:, :, EARLY:])
+        skip_plane = {}
+        for t in (2, 1, 3, 0):
+            tag = "skip_plane%d" % t if t else "skip_then_z"
+            skip_plane[t] = keep.tile([P, EARLY], F32, name="skip_plane%d" % t, tag=tag, align_bytes=64)
+            nc.sync.dma_start(out=skip_plane[t][:], in_=skip_rows[:, t, 0:EARLY])
 
         up = [keep.tile([P, U], F32, name="up%d" % t) for t in range(PACK)]
         for t in range(PACK):
@@ -114,7 +117,7 @@ def tile_picked_unet_none_e_kernel(tc, xT, w1, w2_words, w2_scales, skip, offs, 
                 in_=w_bf[:, t0:t1, :, :].rearrange("p t m j -> p (t m j)"),
             )
 
-        def product(t, cuts):
+        def product(t, cuts, copy=nc.scalar.copy):
             lo, hi = cuts[0], cuts[-1]
             name = "h%d_%d" % (t, lo)
             acc = psum.tile([P, hi - lo], F32, name=name + "_acc", tag="bank")
@@ -129,97 +132,129 @@ def tile_picked_unet_none_e_kernel(tc, xT, w1, w2_words, w2_scales, skip, offs, 
                     stop=True,
                 )
             h = keep.tile([P, hi - lo], F32, name=name)
-            nc.scalar.copy(out=h[:], in_=acc[:])
+            copy(out=h[:], in_=acc[:])
             return h
 
         def scatter(copy, t, lo, hi, values):
             copy(out=up[t][:].indirect(cell_sb[:, lo // LIST_COL : hi // LIST_COL]), in_=values)
 
-        scatter(nc.vector.tensor_copy, 0, 0, SHORT, product(0, [0, SHORT])[:])
+        scatter(nc.vector.tensor_copy, 0, 0, SHORT, product(0, [0, SHORT], nc.vector.tensor_copy)[:])
         scatter(nc.vector.tensor_copy, 0, SHORT, S, product(0, [SHORT, HALF, S])[:])
-        h1, h2, h3 = [product(t, [0, S]) for t in range(1, PACK)]
+        h1, h2 = [product(t, [0, S]) for t in (1, 2)]
         scatter(nc.vector.tensor_copy, 2, 0, S, h2[:])
-        for t, values, lo, hi in [(1, h1, 0, S - SHORT), (3, h3, 0, SHORT), (1, h1, S - SHORT, S), (3, h3, SHORT, S)]:
+        scatter(scalar_copy, 1, 0, SHORT, h1[:, 0:SHORT])
+        h3 = product(3, [0, S])
+        for t, values, lo, hi in [(1, h1, SHORT, S - SHORT), (3, h3, 0, HALF), (1, h1, S - SHORT, S), (3, h3, HALF, S)]:
             scatter(scalar_copy, t, lo, hi, values[:, lo:hi])
 
-        z_bf = keep.tile([P, U, PACK], BF16, name="z_bf", align_bytes=64)
-        nc.gpsimd.tensor_tensor(out=z_bf[:, 0:EARLY, 0], in0=up[0][:, 0:EARLY], in1=skip_early[:], op=ADD)
-        z = keep.tile([P, PACK, U], BF16, name="z", tag="skip_then_z")
+        z_bf = keep.tile([P, EARLY, PACK], BF16, name="z_bf", align_bytes=64)
+        nc.gpsimd.tensor_tensor(out=z_bf[:, :, 0], in0=up[0][:, 0:EARLY], in1=skip_plane[0][:], op=ADD)
+        z = keep.tile([P, PACK - 1, EARLY], BF16, name="z", tag="skip_then_z", align_bytes=64)
 
-        chunks = len(CHUNKS)
-        starts = [sum(CHUNKS[:c]) for c in range(chunks + 1)]
-        chunk_cells = [slice(starts[c], starts[c + 1]) for c in range(chunks)]
+        ident = keep.tile([P, P], F32, name="ident")
+        make_identity(nc, ident[:])
+
+        late_skip = [skip_late[:, t, :] for t in range(PACK)]
+        late_up = [up[t][:, EARLY:] for t in range(PACK)]
+
+        def turn(acc, i, src, t, b, start=False, stop=False):
+            nc.tensor.matmul(
+                out=acc[:, i, :],
+                lhsT=src[t][:, P * b : P * (b + 1)],
+                rhs=ident[:],
+                start=start,
+                stop=stop,
+                is_transpose=True,
+            )
+
+        def paired(name, acc):
+            pairs = keep.tile([P, acc.shape[1] // 2, P, 2], BF16, name=name)
+            nc.scalar.copy(out=pairs[:], in_=acc.rearrange("c (b e) p -> c b p e", e=2))
+            return pairs[:].rearrange("c b p e -> c (b p e)").bitcast(F32)
+
+        low_acc = psum.tile([P, 2 * TURNED, P], F32, name="low_acc", tag="bank")
+        steps = [(src, t, b) for src in (late_skip, late_up) for t in (0, 1) for b in range(TURNED)]
+        for k, (src, t, b) in enumerate(steps):
+            turn(low_acc, 2 * b + t, src, t, b, start=k == 0, stop=k == len(steps) - 1)
+        high_acc = [psum.tile([P, 2, P], F32, name="high_acc%d" % b, tag="bank") for b in range(TURNED)]
+        steps = [(src, t) for src in (late_skip, late_up) for t in (2, 3)]
+        for k, (src, t) in enumerate(steps):
+            for b in range(TURNED):
+                turn(high_acc[b], t - 2, src, t, b, start=k == 0, stop=k == len(steps) - 1)
+        low = paired("low", low_acc[:])
+        highs = [paired("high%d" % b, high_acc[b][:]) for b in range(TURNED)]
+        z_turned = keep.tile([P, TURNED * P, PACK], BF16, name="z_turned", align_bytes=64)
+        z_words = z_turned[:].rearrange("p c t -> p (c t)").bitcast(F32).rearrange("p (c u) -> p c u", u=2)
+        for b in range(TURNED):
+            back = psum.tile([P, 2, P], F32, name="back%d" % b, tag="bank")
+            nc.tensor.transpose(back[:, 0, :], low[:, P * b : P * (b + 1)], ident[:])
+            nc.tensor.transpose(back[:, 1, :], highs[b], ident[:])
+            nc.scalar.copy(out=z_words[:, P * b : P * (b + 1), :], in_=back[:].rearrange("p u c -> p c u"))
+
+        cells = [slice(c0, c0 + n) for c0, n in CHUNKS]
         out_rows = out.rearrange("(a p) v -> p a v", p=P)
 
-        def add(t, cells):
-            nc.vector.tensor_tensor(out=z[:, t, cells], in0=up[t][:, cells], in1=skip_plane[t][:, cells], op=ADD)
-
-        add(1, slice(0, U))
-        add(2, slice(0, starts[2]))
-
-        def add_last(c):
-            add(3, chunk_cells[c])
-            if c >= 2:
-                add(2, chunk_cells[c])
-            if starts[c] >= EARLY:
-                add(0, chunk_cells[c])
+        def add(t, some):
+            nc.vector.tensor_tensor(out=z[:, t - 1, some], in0=up[t][:, some], in1=skip_plane[t][:, some], op=ADD)
 
         def weave(c):
-            copy = nc.scalar.copy if c % 2 else nc.vector.tensor_copy
-            t0 = 1 if starts[c] < EARLY else 0
-            copy(
-                out=z_bf[:, chunk_cells[c], t0:].rearrange("p (c i) t -> p c t i", i=RUN),
-                in_=z[:, t0:, chunk_cells[c]].rearrange("p t (c i) -> p c t i", i=RUN),
+            nc.vector.tensor_copy(
+                out=z_bf[:, cells[c], 1:].rearrange("p (c i) t -> p c t i", i=RUN),
+                in_=z[:, :, cells[c]].rearrange("p t (c i) -> p c t i", i=RUN),
             )
 
-        accs = {}
-
-        def multiply(c):
-            z_codes = keep.tile([P, CHUNKS[c]], U32, name="z_codes%d" % c, align_bytes=64)
-            z_scale = keep.tile([P, CHUNKS[c]], U8, name="z_scale%d" % c, align_bytes=64)
+        def multiply(name, woven, tag=None):
+            n = woven.shape[1]
+            codes = keep.tile([P, n], U32, name=name + "_codes", tag=tag or name + "_codes", align_bytes=64)
+            scale = keep.tile([P, n], U8, name=name + "_scale", align_bytes=64)
             nc.vector.quantize_mx(
-                out=z_codes[:].bitcast(FP8X4),
-                scales=z_scale[:],
-                in_=z_bf[:, chunk_cells[c], :].rearrange("p v t -> p (v t)"),
+                out=codes[:].bitcast(FP8X4), scales=scale[:], in_=woven.rearrange("p v t -> p (v t)")
             )
-            if CHUNKS[c] == NARROW:
-                both = psum.tile([P, N // P, CHUNKS[c]], F32, name="out_acc%d" % c, tag="bank")
-                accs[c] = [both[:]]
+            if n == P:
+                both = psum.tile([P, N // P, n], F32, name=name + "_acc", tag="bank")
+                accs = [both[:]]
                 blocks = [both[:, a, :] for a in range(N // P)]
             else:
-                banks = [
-                    psum.tile([P, 1, CHUNKS[c]], F32, name="out_acc%d_%d" % (c, a), tag="bank") for a in range(N // P)
-                ]
-                accs[c] = [bank[:] for bank in banks]
+                banks = [psum.tile([P, 1, n], F32, name=name + "_acc%d" % a, tag="bank") for a in range(N // P)]
+                accs = [bank[:] for bank in banks]
                 blocks = [bank[:, 0, :] for bank in banks]
             for a in range(N // P):
                 nc.tensor.matmul_mx(
                     out=blocks[a],
                     lhsT=w2_codes[:, 2 * P * a : 2 * P * (a + 1)].bitcast(FP4X4),
                     lhsT_scale=w2_scale[:, P * a : P * (a + 1)],
-                    rhs=z_codes[:].bitcast(FP8X4),
-                    rhs_scale=z_scale[:],
+                    rhs=codes[:].bitcast(FP8X4),
+                    rhs_scale=scale[:],
                     start=True,
                     stop=True,
                 )
+            return accs
 
-        def store(c):
-            res = keep.tile([P, N // P, CHUNKS[c]], F32, name="res%d" % c)
-            for a, acc in enumerate(accs[c]):
+        def store(some, accs, copies):
+            res = keep.tile([P, N // P, some.stop - some.start], F32, name="res%d" % some.start)
+            for a, (acc, copy) in enumerate(zip(accs, copies)):
                 rows = slice(a, a + acc.shape[1])
-                copy = nc.vector.tensor_copy if (c, a) == (chunks - 1, N // P - 1) else nc.scalar.copy
                 copy(out=res[:, rows, :], in_=acc)
-                nc.sync.dma_start(out=out_rows[:, rows, chunk_cells[c]], in_=res[:, rows, :])
+                nc.sync.dma_start(out=out_rows[:, rows, some], in_=res[:, rows, :])
 
-        add_last(0)
-        add_last(1)
+        def chunk(c):
+            return multiply("z%d" % c, z_bf[:, cells[c], :])
+
+        on_scalar, on_vector = nc.scalar.copy, nc.vector.tensor_copy
+        add(2, slice(0, EARLY))
+        add(1, slice(0, EARLY))
+        add(3, cells[0])
+        add(3, cells[1])
         weave(0)
-        for c in range(chunks):
-            if c + 2 < chunks:
-                add_last(c + 2)
-            if c + 1 < chunks:
-                weave(c + 1)
-            multiply(c)
-            if c > 0:
-                store(c - 1)
-        store(chunks - 1)
+        add(3, cells[2])
+        store(cells[0], chunk(0), [on_scalar])
+        weave(1)
+        add(3, cells[3])
+        store(cells[1], chunk(1), [on_scalar, on_scalar])
+        weave(2)
+        weave(3)
+        store(cells[2], chunk(2), [on_scalar, on_scalar])
+        accs_turned = multiply("z_turned", z_turned[:], tag="skip_then_z")
+        accs_last = chunk(3)
+        store(slice(EARLY, U), accs_turned, [on_scalar, on_vector])
+        store(cells[3], accs_last, [on_vector])

@@ -21,7 +21,6 @@ P = 128
 PACK = 4
 LIST_COL = 16
 QUADRANT = 32
-BANKS = 8
 HALF = S // 2
 SHORT = 128
 RUN = 4
@@ -36,7 +35,7 @@ def tile_picked_unet_none_e_kernel(tc, xT, w1, w2_words, w2_scales, skip, offs, 
     nc = tc.nc
     with ExitStack() as ctx:
         keep = ctx.enter_context(tc.tile_pool(name="keep", bufs=1))
-        psum = ctx.enter_context(tc.psum_pool(name="psum", bufs=BANKS))
+        psum = ctx.enter_context(tc.psum_pool(name="psum", bufs=1))
 
         offs_sb = keep.tile([P, S // LIST_COL], U16, name="offs_sb")
         cell_sb = keep.tile([P, S // LIST_COL], U16, name="cell_sb")
@@ -53,6 +52,16 @@ def tile_picked_unet_none_e_kernel(tc, xT, w1, w2_words, w2_scales, skip, offs, 
             nc.sync.dma_start(out=w_raw[a][:], in_=w_rows[:, :, a * H // 2 : (a + 1) * H // 2])
         nc.sync.dma_start(cell_sb[:], cell)
 
+        skip_rows = skip.rearrange("(p t) v -> p t v", t=PACK)
+        skip_late = keep.tile([P, PACK, U - EARLY], F32, name="skip_late")
+        nc.sync.dma_start(out=skip_late[:], in_=skip_rows[:, :, EARLY:])
+        skip_plane = {}
+        for t in (0, 2, 1, 3):
+            width = EARLY if t < 3 else CHUNKS[-1][0]
+            skip_plane[t] = keep.tile([P, width], F32, name="skip_plane%d" % t)
+            nc.sync.dma_start(out=skip_plane[t][:], in_=skip_rows[:, t, 0:width])
+        skip_last = keep.tile([P, 2 * CHUNKS[-1][1]], F32, name="skip_last", tag="skip_then_codes", align_bytes=64)
+        nc.sync.dma_start(out=skip_last[:, 0 : CHUNKS[-1][1]], in_=skip_rows[:, 3, CHUNKS[-1][0] : EARLY])
         w2_codes = keep.tile([P, 2 * N], U8, name="w2_codes", align_bytes=64)
         nc.sync.dma_start(out=w2_codes[:].bitcast(I32), in_=w2_words[0].bitcast(I32))
         w2_scale = keep.tile([P, N], U8, name="w2_scale", align_bytes=64)
@@ -63,16 +72,8 @@ def tile_picked_unet_none_e_kernel(tc, xT, w1, w2_words, w2_scales, skip, offs, 
                 in_=w2_scales[0, 4 * q : 4 * q + 4, :].bitcast(I32),
             )
 
-        skip_rows = skip.rearrange("(p t) v -> p t v", t=PACK)
-        skip_late = keep.tile([P, PACK, U - EARLY], F32, name="skip_late")
-        nc.sync.dma_start(out=skip_late[:], in_=skip_rows[:, :, EARLY:])
-        skip_plane = {}
-        for t in (2, 1, 3, 0):
-            tag = "skip_plane%d" % t if t else "skip_then_z"
-            skip_plane[t] = keep.tile([P, EARLY], F32, name="skip_plane%d" % t, tag=tag, align_bytes=64)
-            nc.sync.dma_start(out=skip_plane[t][:], in_=skip_rows[:, t, 0:EARLY])
 
-        up = [keep.tile([P, U], F32, name="up%d" % t) for t in range(PACK)]
+        up = [keep.tile([P, U], F32, name="up%d" % t, tag="up%d" % t) for t in range(PACK)]
         for t in range(PACK):
             nc.vector.memset(up[t][:], 0.0)
 
@@ -120,7 +121,7 @@ def tile_picked_unet_none_e_kernel(tc, xT, w1, w2_words, w2_scales, skip, offs, 
         def product(t, cuts, copy=nc.scalar.copy):
             lo, hi = cuts[0], cuts[-1]
             name = "h%d_%d" % (t, lo)
-            acc = psum.tile([P, hi - lo], F32, name=name + "_acc", tag="bank")
+            acc = psum.tile([P, hi - lo], F32, name=name + "_acc", tag="bank%d" % (t + (lo + t > 0)))
             for c0, c1 in zip(cuts, cuts[1:]):
                 nc.tensor.matmul_mx(
                     out=acc[:, c0 - lo : c1 - lo],
@@ -149,7 +150,6 @@ def tile_picked_unet_none_e_kernel(tc, xT, w1, w2_words, w2_scales, skip, offs, 
 
         z_bf = keep.tile([P, EARLY, PACK], BF16, name="z_bf", align_bytes=64)
         nc.gpsimd.tensor_tensor(out=z_bf[:, :, 0], in0=up[0][:, 0:EARLY], in1=skip_plane[0][:], op=ADD)
-        z = keep.tile([P, PACK - 1, EARLY], BF16, name="z", tag="skip_then_z", align_bytes=64)
 
         ident = keep.tile([P, P], F32, name="ident")
         make_identity(nc, ident[:])
@@ -172,11 +172,11 @@ def tile_picked_unet_none_e_kernel(tc, xT, w1, w2_words, w2_scales, skip, offs, 
             nc.scalar.copy(out=pairs[:], in_=acc.rearrange("c (b e) p -> c b p e", e=2))
             return pairs[:].rearrange("c b p e -> c (b p e)").bitcast(F32)
 
-        low_acc = psum.tile([P, 2 * TURNED, P], F32, name="low_acc", tag="bank")
+        low_acc = psum.tile([P, 2 * TURNED, P], F32, name="low_acc", tag="bank3")
         steps = [(src, t, b) for src in (late_skip, late_up) for t in (0, 1) for b in range(TURNED)]
         for k, (src, t, b) in enumerate(steps):
             turn(low_acc, 2 * b + t, src, t, b, start=k == 0, stop=k == len(steps) - 1)
-        high_acc = [psum.tile([P, 2, P], F32, name="high_acc%d" % b, tag="bank") for b in range(TURNED)]
+        high_acc = [psum.tile([P, 2, P], F32, name="high_acc%d" % b, tag=("bank4", "bank2")[b]) for b in range(TURNED)]
         steps = [(src, t) for src in (late_skip, late_up) for t in (2, 3)]
         for k, (src, t) in enumerate(steps):
             for b in range(TURNED):
@@ -186,16 +186,18 @@ def tile_picked_unet_none_e_kernel(tc, xT, w1, w2_words, w2_scales, skip, offs, 
         z_turned = keep.tile([P, TURNED * P, PACK], BF16, name="z_turned", align_bytes=64)
         z_words = z_turned[:].rearrange("p c t -> p (c t)").bitcast(F32).rearrange("p (c u) -> p c u", u=2)
         for b in range(TURNED):
-            back = psum.tile([P, 2, P], F32, name="back%d" % b, tag="bank")
+            back = psum.tile([P, 2, P], F32, name="back%d" % b, tag="bank%d" % (5 + b))
             nc.tensor.transpose(back[:, 0, :], low[:, P * b : P * (b + 1)], ident[:])
             nc.tensor.transpose(back[:, 1, :], highs[b], ident[:])
             nc.scalar.copy(out=z_words[:, P * b : P * (b + 1), :], in_=back[:].rearrange("p u c -> p c u"))
 
+        z = keep.tile([P, PACK - 1, EARLY], BF16, name="z", tag="up0")
         cells = [slice(c0, c0 + n) for c0, n in CHUNKS]
         out_rows = out.rearrange("(a p) v -> p a v", p=P)
 
-        def add(t, some):
-            nc.vector.tensor_tensor(out=z[:, t - 1, some], in0=up[t][:, some], in1=skip_plane[t][:, some], op=ADD)
+        def add(t, some, other=None):
+            other = skip_plane[t][:, some] if other is None else other
+            nc.vector.tensor_tensor(out=z[:, t - 1, some], in0=up[t][:, some], in1=other, op=ADD)
 
         def weave(c):
             nc.vector.tensor_copy(
@@ -203,7 +205,7 @@ def tile_picked_unet_none_e_kernel(tc, xT, w1, w2_words, w2_scales, skip, offs, 
                 in_=z[:, :, cells[c]].rearrange("p t (c i) -> p c t i", i=RUN),
             )
 
-        def multiply(name, woven, tag=None):
+        def multiply(name, woven, tags, tag=None):
             n = woven.shape[1]
             codes = keep.tile([P, n], U32, name=name + "_codes", tag=tag or name + "_codes", align_bytes=64)
             scale = keep.tile([P, n], U8, name=name + "_scale", align_bytes=64)
@@ -211,11 +213,11 @@ def tile_picked_unet_none_e_kernel(tc, xT, w1, w2_words, w2_scales, skip, offs, 
                 out=codes[:].bitcast(FP8X4), scales=scale[:], in_=woven.rearrange("p v t -> p (v t)")
             )
             if n == P:
-                both = psum.tile([P, N // P, n], F32, name=name + "_acc", tag="bank")
+                both = psum.tile([P, N // P, n], F32, name=name + "_acc", tag=tags[0])
                 accs = [both[:]]
                 blocks = [both[:, a, :] for a in range(N // P)]
             else:
-                banks = [psum.tile([P, 1, n], F32, name=name + "_acc%d" % a, tag="bank") for a in range(N // P)]
+                banks = [psum.tile([P, 1, n], F32, name=name + "_acc%d" % a, tag=tags[a]) for a in range(N // P)]
                 accs = [bank[:] for bank in banks]
                 blocks = [bank[:, 0, :] for bank in banks]
             for a in range(N // P):
@@ -237,8 +239,10 @@ def tile_picked_unet_none_e_kernel(tc, xT, w1, w2_words, w2_scales, skip, offs, 
                 copy(out=res[:, rows, :], in_=acc)
                 nc.sync.dma_start(out=out_rows[:, rows, some], in_=res[:, rows, :])
 
+        out_banks = [["bank2"], ["bank5", "bank6"], ["bank2", "bank5"], ["bank6"]]
+
         def chunk(c):
-            return multiply("z%d" % c, z_bf[:, cells[c], :])
+            return multiply("z%d" % c, z_bf[:, cells[c], :], out_banks[c])
 
         on_scalar, on_vector = nc.scalar.copy, nc.vector.tensor_copy
         add(2, slice(0, EARLY))
@@ -246,15 +250,16 @@ def tile_picked_unet_none_e_kernel(tc, xT, w1, w2_words, w2_scales, skip, offs, 
         add(3, cells[0])
         add(3, cells[1])
         weave(0)
-        add(3, cells[2])
-        store(cells[0], chunk(0), [on_scalar])
         weave(1)
-        add(3, cells[3])
+        store(cells[0], chunk(0), [on_scalar])
+        add(3, cells[2])
         store(cells[1], chunk(1), [on_scalar, on_scalar])
+        add(3, cells[3], skip_last[:, 0 : CHUNKS[-1][1]])
         weave(2)
+        accs_turned = multiply("z_turned", z_turned[:], ["bank3", "bank4"], tag="skip_then_codes")
+        accs_2 = chunk(2)
         weave(3)
-        store(cells[2], chunk(2), [on_scalar, on_scalar])
-        accs_turned = multiply("z_turned", z_turned[:], tag="skip_then_z")
         accs_last = chunk(3)
-        store(slice(EARLY, U), accs_turned, [on_scalar, on_vector])
+        store(slice(EARLY, U), accs_turned, [on_scalar, on_scalar])
+        store(cells[2], accs_2, [on_vector, on_scalar])
         store(cells[3], accs_last, [on_vector])

@@ -56,7 +56,7 @@ def tile_picked_unet_none_e_kernel(tc, xT, w1, w2_words, w2_scales, skip, offs, 
         skip_late = keep.tile([P, PACK, U - EARLY], F32, name="skip_late")
         nc.sync.dma_start(out=skip_late[:], in_=skip_rows[:, :, EARLY:])
         skip_plane = {}
-        for t in (0, 2, 1, 3):
+        for t in (0, 1, 2, 3):
             width = EARLY if t < 3 else CHUNKS[-1][0]
             skip_plane[t] = keep.tile([P, width], F32, name="skip_plane%d" % t)
             nc.sync.dma_start(out=skip_plane[t][:], in_=skip_rows[:, t, 0:width])
@@ -118,10 +118,11 @@ def tile_picked_unet_none_e_kernel(tc, xT, w1, w2_words, w2_scales, skip, offs, 
                 in_=w_bf[:, t0:t1, :, :].rearrange("p t m j -> p (t m j)"),
             )
 
-        def product(t, cuts, copy=nc.scalar.copy):
+        h = [keep.tile([P, S], F32, name="h%d" % t) for t in range(PACK)]
+
+        def product(t, cuts, bank, copy):
             lo, hi = cuts[0], cuts[-1]
-            name = "h%d_%d" % (t, lo)
-            acc = psum.tile([P, hi - lo], F32, name=name + "_acc", tag="bank%d" % (t + (lo + t > 0)))
+            acc = psum.tile([P, hi - lo], F32, name="h%d_%d_acc" % (t, lo), tag="bank%d" % bank)
             for c0, c1 in zip(cuts, cuts[1:]):
                 nc.tensor.matmul_mx(
                     out=acc[:, c0 - lo : c1 - lo],
@@ -132,21 +133,25 @@ def tile_picked_unet_none_e_kernel(tc, xT, w1, w2_words, w2_scales, skip, offs, 
                     start=True,
                     stop=True,
                 )
-            h = keep.tile([P, hi - lo], F32, name=name)
-            copy(out=h[:], in_=acc[:])
-            return h
+            copy(out=h[t][:, lo:hi], in_=acc[:])
 
-        def scatter(copy, t, lo, hi, values):
-            copy(out=up[t][:].indirect(cell_sb[:, lo // LIST_COL : hi // LIST_COL]), in_=values)
+        def scatter(copy, t, lo, hi):
+            copy(out=up[t][:].indirect(cell_sb[:, lo // LIST_COL : hi // LIST_COL]), in_=h[t][:, lo:hi])
 
-        scatter(nc.vector.tensor_copy, 0, 0, SHORT, product(0, [0, SHORT], nc.vector.tensor_copy)[:])
-        scatter(nc.vector.tensor_copy, 0, SHORT, S, product(0, [SHORT, HALF, S])[:])
-        h1, h2 = [product(t, [0, S]) for t in (1, 2)]
-        scatter(nc.vector.tensor_copy, 2, 0, S, h2[:])
-        scatter(scalar_copy, 1, 0, SHORT, h1[:, 0:SHORT])
-        h3 = product(3, [0, S])
-        for t, values, lo, hi in [(1, h1, SHORT, S - SHORT), (3, h3, 0, HALF), (1, h1, S - SHORT, S), (3, h3, HALF, S)]:
-            scatter(scalar_copy, t, lo, hi, values[:, lo:hi])
+        on_scalar, on_vector = nc.scalar.copy, nc.vector.tensor_copy
+        product(0, [0, SHORT], 0, on_vector)
+        product(1, [0, SHORT], 1, on_scalar)
+        product(0, [SHORT, HALF, S], 2, on_scalar)
+        scatter(on_vector, 0, 0, SHORT)
+        scatter(scalar_copy, 1, 0, SHORT)
+        product(2, [0, HALF], 3, on_vector)
+        scatter(on_vector, 0, SHORT, S)
+        product(1, [SHORT, HALF, S], 4, on_scalar)
+        product(2, [HALF, S], 5, on_scalar)
+        product(3, [0, S], 6, on_scalar)
+        scatter(on_vector, 2, 0, S)
+        for t, lo, hi in [(1, SHORT, S - SHORT), (3, 0, SHORT), (1, S - SHORT, S), (3, SHORT, S)]:
+            scatter(scalar_copy, t, lo, hi)
 
         z_bf = keep.tile([P, EARLY, PACK], BF16, name="z_bf", align_bytes=64)
         nc.gpsimd.tensor_tensor(out=z_bf[:, :, 0], in0=up[0][:, 0:EARLY], in1=skip_plane[0][:], op=ADD)
@@ -172,11 +177,11 @@ def tile_picked_unet_none_e_kernel(tc, xT, w1, w2_words, w2_scales, skip, offs, 
             nc.scalar.copy(out=pairs[:], in_=acc.rearrange("c (b e) p -> c b p e", e=2))
             return pairs[:].rearrange("c b p e -> c (b p e)").bitcast(F32)
 
-        low_acc = psum.tile([P, 2 * TURNED, P], F32, name="low_acc", tag="bank3")
+        low_acc = psum.tile([P, 2 * TURNED, P], F32, name="low_acc", tag="bank5")
         steps = [(src, t, b) for src in (late_skip, late_up) for t in (0, 1) for b in range(TURNED)]
         for k, (src, t, b) in enumerate(steps):
             turn(low_acc, 2 * b + t, src, t, b, start=k == 0, stop=k == len(steps) - 1)
-        high_acc = [psum.tile([P, 2, P], F32, name="high_acc%d" % b, tag=("bank4", "bank2")[b]) for b in range(TURNED)]
+        high_acc = [psum.tile([P, 2, P], F32, name="high_acc%d" % b, tag=("bank6", "bank4")[b]) for b in range(TURNED)]
         steps = [(src, t) for src in (late_skip, late_up) for t in (2, 3)]
         for k, (src, t) in enumerate(steps):
             for b in range(TURNED):
@@ -186,7 +191,7 @@ def tile_picked_unet_none_e_kernel(tc, xT, w1, w2_words, w2_scales, skip, offs, 
         z_turned = keep.tile([P, TURNED * P, PACK], BF16, name="z_turned", align_bytes=64)
         z_words = z_turned[:].rearrange("p c t -> p (c t)").bitcast(F32).rearrange("p (c u) -> p c u", u=2)
         for b in range(TURNED):
-            back = psum.tile([P, 2, P], F32, name="back%d" % b, tag="bank%d" % (5 + b))
+            back = psum.tile([P, 2, P], F32, name="back%d" % b, tag="bank%d" % b)
             nc.tensor.transpose(back[:, 0, :], low[:, P * b : P * (b + 1)], ident[:])
             nc.tensor.transpose(back[:, 1, :], highs[b], ident[:])
             nc.scalar.copy(out=z_words[:, P * b : P * (b + 1), :], in_=back[:].rearrange("p u c -> p c u"))
@@ -205,14 +210,19 @@ def tile_picked_unet_none_e_kernel(tc, xT, w1, w2_words, w2_scales, skip, offs, 
                 in_=z[:, :, cells[c]].rearrange("p t (c i) -> p c t i", i=RUN),
             )
 
-        def multiply(name, woven, tags, tag=None):
+        def quantised(name, woven, tag=None):
             n = woven.shape[1]
             codes = keep.tile([P, n], U32, name=name + "_codes", tag=tag or name + "_codes", align_bytes=64)
             scale = keep.tile([P, n], U8, name=name + "_scale", align_bytes=64)
             nc.vector.quantize_mx(
                 out=codes[:].bitcast(FP8X4), scales=scale[:], in_=woven.rearrange("p v t -> p (v t)")
             )
-            if n == P:
+            return codes, scale
+
+        def multiply(name, operand, tags):
+            codes, scale = operand
+            n = codes.shape[1]
+            if len(tags) == 1:
                 both = psum.tile([P, N // P, n], F32, name=name + "_acc", tag=tags[0])
                 accs = [both[:]]
                 blocks = [both[:, a, :] for a in range(N // P)]
@@ -239,14 +249,13 @@ def tile_picked_unet_none_e_kernel(tc, xT, w1, w2_words, w2_scales, skip, offs, 
                 copy(out=res[:, rows, :], in_=acc)
                 nc.sync.dma_start(out=out_rows[:, rows, some], in_=res[:, rows, :])
 
-        out_banks = [["bank2"], ["bank5", "bank6"], ["bank2", "bank5"], ["bank6"]]
+        out_banks = [["bank4"], ["bank0", "bank1"], ["bank4", "bank0"], ["bank1", "bank5"]]
 
         def chunk(c):
-            return multiply("z%d" % c, z_bf[:, cells[c], :], out_banks[c])
+            return multiply("z%d" % c, quantised("z%d" % c, z_bf[:, cells[c], :]), out_banks[c])
 
-        on_scalar, on_vector = nc.scalar.copy, nc.vector.tensor_copy
-        add(2, slice(0, EARLY))
         add(1, slice(0, EARLY))
+        add(2, slice(0, EARLY))
         add(3, cells[0])
         add(3, cells[1])
         weave(0)
@@ -256,10 +265,10 @@ def tile_picked_unet_none_e_kernel(tc, xT, w1, w2_words, w2_scales, skip, offs, 
         store(cells[1], chunk(1), [on_scalar, on_scalar])
         add(3, cells[3], skip_last[:, 0 : CHUNKS[-1][1]])
         weave(2)
-        accs_turned = multiply("z_turned", z_turned[:], ["bank3", "bank4"], tag="skip_then_codes")
-        accs_2 = chunk(2)
+        accs_turned = multiply("z_turned", quantised("z_turned", z_turned[:], "skip_then_codes"), ["bank5", "bank6"])
         weave(3)
-        accs_last = chunk(3)
-        store(slice(EARLY, U), accs_turned, [on_scalar, on_scalar])
-        store(cells[2], accs_2, [on_vector, on_scalar])
-        store(cells[3], accs_last, [on_vector])
+        accs_2 = chunk(2)
+        codes_last = quantised("z3", z_bf[:, cells[3], :])
+        store(slice(EARLY, U), accs_turned, [on_scalar, on_vector])
+        store(cells[2], accs_2, [on_scalar, on_vector])
+        store(cells[3], multiply("z3", codes_last, out_banks[3]), [on_scalar, on_vector])

@@ -23,7 +23,7 @@ LIST_COL = 16
 QUADRANT = 32
 HALF = S // 2
 SHORT = 128
-RUN = 4
+RUN = 2
 DEAL_CUT = 104
 
 EARLY = 768

@@ -104,13 +104,13 @@ def tile_picked_unet_none_e_kernel(tc, xT, w1, w2_words, w2_scales, skip, offs, 
         def deal(copy, lo, hi):
             a = lo // (P // 2)
             copy(
-                out=w_bf[:, :, lo:hi, :].rearrange("p t m j -> p m j t"),
-                in_=w_raw[a][:].rearrange("p j (m t) -> p m j t", t=PACK)[:, lo - a * P // 2 : hi - a * P // 2, :, :],
+                out=w_bf[:, :, lo:hi, :].rearrange("p t m (u e) -> p m u t e", e=2),
+                in_=w_raw[a][:].rearrange("p (u e) (m t) -> p m u t e", e=2, t=PACK)[:, lo - a * P // 2 : hi - a * P // 2],
             )
 
-        deal(scalar_copy, 0, P // 2)
+        deal(nc.scalar.copy, 0, P // 2)
         deal(nc.vector.tensor_copy, P // 2, DEAL_CUT)
-        deal(scalar_copy, DEAL_CUT, P)
+        deal(nc.scalar.copy, DEAL_CUT, P)
         for t0, t1 in [(0, 1), (1, 2), (2, PACK)]:
             nc.vector.quantize_mx(
                 out=w_codes[:, P * t0 : P * t1].bitcast(FP8X4),

from contextlib import ExitStack

import concourse.mybir as mybir
from concourse.masks import make_identity

K, T, S, H, N, U = 512, 2048, 512, 512, 256, 1024
FLOPS = 2 * K * H * S + 2 * H * N * U

F32 = mybir.dt.float32
BF16 = mybir.dt.bfloat16
I32 = mybir.dt.int32
U32 = mybir.dt.uint32
U16 = mybir.dt.uint16
U8 = mybir.dt.uint8
FP8X4 = mybir.dt.float8_e4m3fn_x4
FP4X4 = mybir.dt.float4_e2m1fn_x4
ADD = mybir.AluOpType.add
COPY = mybir.ActivationFunctionType.Copy

P = 128
PACK = 4
LIST_COL = 16
QUADRANT = 32
HALF = S // 2
SHORT = 128
RUN = 2
DEAL_CUT = 104

EARLY = 768
TURNED = (U - EARLY) // P
CHUNKS = [(0, 128), (128, 256), (384, 256), (640, 128)]


def tile_picked_unet_none_e_kernel(tc, xT, w1, w2_words, w2_scales, skip, offs, cell, out):
    nc = tc.nc
    with ExitStack() as ctx:
        keep = ctx.enter_context(tc.tile_pool(name="keep", bufs=1))
        psum = ctx.enter_context(tc.psum_pool(name="psum", bufs=1))

        offs_sb = keep.tile([P, S // LIST_COL], U16, name="offs_sb")
        cell_sb = keep.tile([P, S // LIST_COL], U16, name="cell_sb")

        x_rows = xT.rearrange("(p j) c -> p j c", j=PACK)
        x_plane = [keep.tile([P, T], F32, name="x_plane%d" % j) for j in range(PACK)]
        for j in range(PACK):
            nc.sync.dma_start(out=x_plane[j][:], in_=x_rows[:, j, :])
            if j == 0:
                nc.sync.dma_start(offs_sb[:], offs)
        w_rows = w1.rearrange("(p j) c -> p j c", j=PACK)
        w_raw = [keep.tile([P, PACK, H // 2], F32, name="w_raw%d" % a) for a in range(2)]
        for a in range(2):
            nc.sync.dma_start(out=w_raw[a][:], in_=w_rows[:, :, a * H // 2 : (a + 1) * H // 2])
        nc.sync.dma_start(cell_sb[:], cell)

        skip_rows = skip.rearrange("(p t) v -> p t v", t=PACK)
        skip_late = keep.tile([P, PACK, U - EARLY], F32, name="skip_late")
        nc.sync.dma_start(out=skip_late[:], in_=skip_rows[:, :, EARLY:])
        skip_plane = {}
        for t in (0, 1, 2, 3):
            width = EARLY if t < 3 else CHUNKS[-1][0]
            skip_plane[t] = keep.tile([P, width], F32, name="skip_plane%d" % t)
            nc.sync.dma_start(out=skip_plane[t][:], in_=skip_rows[:, t, 0:width])
        skip_last = keep.tile([P, 2 * CHUNKS[-1][1]], F32, name="skip_last", tag="skip_then_codes", align_bytes=64)
        nc.sync.dma_start(out=skip_last[:, 0 : CHUNKS[-1][1]], in_=skip_rows[:, 3, CHUNKS[-1][0] : EARLY])
        w2_codes = keep.tile([P, 2 * N], U8, name="w2_codes", align_bytes=64)
        nc.sync.dma_start(out=w2_codes[:].bitcast(I32), in_=w2_words[0].bitcast(I32))
        w2_scale = keep.tile([P, N], U8, name="w2_scale", align_bytes=64)
        nc.vector.memset(w2_scale[:].bitcast(I32), 0)
        for q in range(P // QUADRANT):
            nc.sync.dma_start(
                out=w2_scale[QUADRANT * q : QUADRANT * q + 4, :].bitcast(I32),
                in_=w2_scales[0, 4 * q : 4 * q + 4, :].bitcast(I32),
            )


        up = [keep.tile([P, U], F32, name="up%d" % t, tag="up%d" % t) for t in range(PACK)]
        for t in range(PACK):
            nc.vector.memset(up[t][:], 0.0)

        def scalar_copy(out, in_):
            nc.scalar.activation(out=out, in_=in_, func=COPY)

        x_bf = [keep.tile([P, HALF, PACK], BF16, name="x_bf%d" % a, align_bytes=64) for a in range(2)]
        x_pair = [keep.tile([P, 2, HALF], BF16, name="x_pair%d" % e) for e in range(2)]
        for j in range(PACK):
            nc.vector.tensor_copy(x_bf[0][:, :, j], x_plane[j][:].indirect(offs_sb[:, 0 : HALF // LIST_COL]))
            scalar_copy(out=x_pair[j // 2][:, j % 2, :], in_=x_plane[j][:].indirect(offs_sb[:, HALF // LIST_COL :]))
            if j % 2:
                nc.vector.tensor_copy(x_bf[1][:, :, j - 1 : j + 1], x_pair[j // 2][:].rearrange("p e s -> p s e"))
        x_codes = keep.tile([P, S], U32, name="x_codes", align_bytes=64)
        x_scale = keep.tile([P, S], U8, name="x_scale", align_bytes=64)
        for a in range(2):
            points = slice(a * HALF, (a + 1) * HALF)
            nc.vector.quantize_mx(
                out=x_codes[:, points].bitcast(FP8X4),
                scales=x_scale[:, points],
                in_=x_bf[a][:].rearrange("p s j -> p (s j)"),
            )

        w_bf = keep.tile([P, PACK, P, PACK], BF16, name="w_bf", align_bytes=64)
        w_codes = keep.tile([P, H], U32, name="w_codes", align_bytes=64)
        w_scale = keep.tile([P, H], U8, name="w_scale", align_bytes=64)

        def deal(copy, lo, hi):
            a = lo // (P // 2)
            copy(
                out=w_bf[:, :, lo:hi, :].rearrange("p t m (u e) -> p m u t e", e=2),
                in_=w_raw[a][:].rearrange("p (u e) (m t) -> p m u t e", e=2, t=PACK)[:, lo - a * P // 2 : hi - a * P // 2],
            )

        deal(nc.scalar.copy, 0, P // 2)
        deal(nc.vector.tensor_copy, P // 2, DEAL_CUT)
        deal(nc.scalar.copy, DEAL_CUT, P)
        for t0, t1 in [(0, 1), (1, 2), (2, PACK)]:
            nc.vector.quantize_mx(
                out=w_codes[:, P * t0 : P * t1].bitcast(FP8X4),
                scales=w_scale[:, P * t0 : P * t1],
                in_=w_bf[:, t0:t1, :, :].rearrange("p t m j -> p (t m j)"),
            )

        h = [keep.tile([P, S], F32, name="h%d" % t) for t in range(PACK)]

        def product(t, cuts, bank, copy):
            lo, hi = cuts[0], cuts[-1]
            acc = psum.tile([P, hi - lo], F32, name="h%d_%d_acc" % (t, lo), tag="bank%d" % bank)
            for c0, c1 in zip(cuts, cuts[1:]):
                nc.tensor.matmul_mx(
                    out=acc[:, c0 - lo : c1 - lo],
                    lhsT=w_codes[:, P * t : P * (t + 1)].bitcast(FP8X4),
                    lhsT_scale=w_scale[:, P * t : P * (t + 1)],
                    rhs=x_codes[:, c0:c1].bitcast(FP8X4),
                    rhs_scale=x_scale[:, c0:c1],
                    start=True,
                    stop=True,
                )
            copy(out=h[t][:, lo:hi], in_=acc[:])

        def scatter(copy, t, lo, hi):
            copy(out=up[t][:].indirect(cell_sb[:, lo // LIST_COL : hi // LIST_COL]), in_=h[t][:, lo:hi])

        on_scalar, on_vector = nc.scalar.copy, nc.vector.tensor_copy
        product(0, [0, SHORT], 0, on_vector)
        product(1, [0, SHORT], 1, on_scalar)
        product(0, [SHORT, HALF, S], 2, on_scalar)
        scatter(on_vector, 0, 0, SHORT)
        scatter(scalar_copy, 1, 0, SHORT)
        product(2, [0, HALF], 3, on_vector)
        scatter(on_vector, 0, SHORT, S)
        product(1, [SHORT, HALF, S], 4, on_scalar)
        product(2, [HALF, S], 5, on_scalar)
        product(3, [0, S], 6, on_scalar)
        scatter(on_vector, 2, 0, S)
        for t, lo, hi in [(1, SHORT, S - SHORT), (3, 0, SHORT), (1, S - SHORT, S), (3, SHORT, S)]:
            scatter(scalar_copy, t, lo, hi)

        z_bf = keep.tile([P, EARLY, PACK], BF16, name="z_bf", align_bytes=64)
        nc.gpsimd.tensor_tensor(out=z_bf[:, :, 0], in0=up[0][:, 0:EARLY], in1=skip_plane[0][:], op=ADD)

        ident = keep.tile([P, P], F32, name="ident")
        make_identity(nc, ident[:])

        late_skip = [skip_late[:, t, :] for t in range(PACK)]
        late_up = [up[t][:, EARLY:] for t in range(PACK)]

        def turn(acc, i, src, t, b, start=False, stop=False):
            nc.tensor.matmul(
                out=acc[:, i, :],
                lhsT=src[t][:, P * b : P * (b + 1)],
                rhs=ident[:],
                start=start,
                stop=stop,
                is_transpose=True,
            )

        def paired(name, acc):
            pairs = keep.tile([P, acc.shape[1] // 2, P, 2], BF16, name=name)
            nc.scalar.copy(out=pairs[:], in_=acc.rearrange("c (b e) p -> c b p e", e=2))
            return pairs[:].rearrange("c b p e -> c (b p e)").bitcast(F32)

        low_acc = psum.tile([P, 2 * TURNED, P], F32, name="low_acc", tag="bank5")
        steps = [(src, t, b) for src in (late_skip, late_up) for t in (0, 1) for b in range(TURNED)]
        for k, (src, t, b) in enumerate(steps):
            turn(low_acc, 2 * b + t, src, t, b, start=k == 0, stop=k == len(steps) - 1)
        high_acc = [psum.tile([P, 2, P], F32, name="high_acc%d" % b, tag=("bank6", "bank4")[b]) for b in range(TURNED)]
        steps = [(src, t) for src in (late_skip, late_up) for t in (2, 3)]
        for k, (src, t) in enumerate(steps):
            for b in range(TURNED):
                turn(high_acc[b], t - 2, src, t, b, start=k == 0, stop=k == len(steps) - 1)
        low = paired("low", low_acc[:])
        highs = [paired("high%d" % b, high_acc[b][:]) for b in range(TURNED)]
        z_turned = keep.tile([P, TURNED * P, PACK], BF16, name="z_turned", align_bytes=64)
        z_words = z_turned[:].rearrange("p c t -> p (c t)").bitcast(F32).rearrange("p (c u) -> p c u", u=2)
        for b in range(TURNED):
            back = psum.tile([P, 2, P], F32, name="back%d" % b, tag="bank%d" % b)
            nc.tensor.transpose(back[:, 0, :], low[:, P * b : P * (b + 1)], ident[:])
            nc.tensor.transpose(back[:, 1, :], highs[b], ident[:])
            nc.scalar.copy(out=z_words[:, P * b : P * (b + 1), :], in_=back[:].rearrange("p u c -> p c u"))

        z = keep.tile([P, PACK - 1, EARLY], BF16, name="z", tag="up0")
        cells = [slice(c0, c0 + n) for c0, n in CHUNKS]
        out_rows = out.rearrange("(a p) v -> p a v", p=P)

        def add(t, some, other=None):
            other = skip_plane[t][:, some] if other is None else other
            nc.vector.tensor_tensor(out=z[:, t - 1, some], in0=up[t][:, some], in1=other, op=ADD)

        def weave(c):
            nc.vector.tensor_copy(
                out=z_bf[:, cells[c], 1:].rearrange("p (c i) t -> p c t i", i=RUN),
                in_=z[:, :, cells[c]].rearrange("p t (c i) -> p c t i", i=RUN),
            )

        def quantised(name, woven, tag=None):
            n = woven.shape[1]
            codes = keep.tile([P, n], U32, name=name + "_codes", tag=tag or name + "_codes", align_bytes=64)
            scale = keep.tile([P, n], U8, name=name + "_scale", align_bytes=64)
            nc.vector.quantize_mx(
                out=codes[:].bitcast(FP8X4), scales=scale[:], in_=woven.rearrange("p v t -> p (v t)")
            )
            return codes, scale

        def multiply(name, operand, tags):
            codes, scale = operand
            n = codes.shape[1]
            if len(tags) == 1:
                both = psum.tile([P, N // P, n], F32, name=name + "_acc", tag=tags[0])
                accs = [both[:]]
                blocks = [both[:, a, :] for a in range(N // P)]
            else:
                banks = [psum.tile([P, 1, n], F32, name=name + "_acc%d" % a, tag=tags[a]) for a in range(N // P)]
                accs = [bank[:] for bank in banks]
                blocks = [bank[:, 0, :] for bank in banks]
            for a in range(N // P):
                nc.tensor.matmul_mx(
                    out=blocks[a],
                    lhsT=w2_codes[:, 2 * P * a : 2 * P * (a + 1)].bitcast(FP4X4),
                    lhsT_scale=w2_scale[:, P * a : P * (a + 1)],
                    rhs=codes[:].bitcast(FP8X4),
                    rhs_scale=scale[:],
                    start=True,
                    stop=True,
                )
            return accs

        def store(some, accs, copies):
            res = keep.tile([P, N // P, some.stop - some.start], F32, name="res%d" % some.start)
            for a, (acc, copy) in enumerate(zip(accs, copies)):
                rows = slice(a, a + acc.shape[1])
                copy(out=res[:, rows, :], in_=acc)
                nc.sync.dma_start(out=out_rows[:, rows, some], in_=res[:, rows, :])

        out_banks = [["bank4"], ["bank0", "bank1"], ["bank4", "bank0"], ["bank1", "bank5"]]

        def chunk(c):
            return multiply("z%d" % c, quantised("z%d" % c, z_bf[:, cells[c], :]), out_banks[c])

        add(1, slice(0, EARLY))
        add(2, slice(0, EARLY))
        add(3, cells[0])
        add(3, cells[1])
        weave(0)
        weave(1)
        store(cells[0], chunk(0), [on_scalar])
        add(3, cells[2])
        store(cells[1], chunk(1), [on_scalar, on_scalar])
        add(3, cells[3], skip_last[:, 0 : CHUNKS[-1][1]])
        weave(2)
        accs_turned = multiply("z_turned", quantised("z_turned", z_turned[:], "skip_then_codes"), ["bank5", "bank6"])
        weave(3)
        accs_2 = chunk(2)
        codes_last = quantised("z3", z_bf[:, cells[3], :])
        store(slice(EARLY, U), accs_turned, [on_scalar, on_vector])
        store(cells[2], accs_2, [on_scalar, on_vector])
        store(cells[3], multiply("z3", codes_last, out_banks[3]), [on_scalar, on_vector])
